import numpy as np, ml_dtypes
CORES = [9,25,41,57]
N = 4
import mx_ref
BF = ml_dtypes.bfloat16
def gentries(a):
    return np.ascontiguousarray(a.reshape(8, 16, -1).transpose(0, 2, 1)).reshape(8, -1)
def gtable(e):
    e = np.asarray(e); return np.ascontiguousarray(e.reshape(8, -1, 16).transpose(0, 2, 1)).reshape(128, -1).astype(np.int32)
def gcols(t, e):
    v = np.concatenate([t.reshape(8, 16, -1, 4), np.zeros((8, 16, 1, 4), BF)], axis=2)
    return np.ascontiguousarray(np.stack([v[g][:, e[g]] for g in range(8)])).reshape(128, -1)
def tile(rs):
    return np.stack(rs, axis=2).reshape(128, -1).astype(BF)
def pick(q, e):
    c = np.concatenate([q[0].reshape(128, -1, 4), np.zeros((128, 1, 4), np.uint8)], axis=1); s = np.concatenate([q[1], np.ones((16, 1), np.uint8)], axis=1)
    return (np.ascontiguousarray(c[:, e].reshape(128, -1)), np.ascontiguousarray(s[:, e]))
def join(*qs):
    return (np.concatenate([q[0] for q in qs], axis=1), np.concatenate([q[1] for q in qs], axis=1))
def put(q, e, v):
    c, s = q[0].reshape(128, -1, 4).copy(), q[1].copy(); c[:, e] = v[0].reshape(128, -1, 4); s[:, e] = v[1]
    return (c.reshape(128, -1), s)
def pk(c, s):
    return (np.ascontiguousarray(c), mx_ref.live(s))
def emit(q):
    return q[0], q[1]
def packed(v, rng):
    q = [mx_ref.quantize(np.ascontiguousarray(v[r])) for r in range(N)]
    return np.stack([a for a, b in q]), np.stack([mx_ref.plane(b, rng) for a, b in q])
def values_of_codes():
    e, c = np.zeros((128, 128, 4), np.float32), np.zeros((128, 2, 4), np.uint8)
    e[np.arange(128), np.arange(128), 0] = 1
    c[:127, :, 0] = np.arange(256).reshape(2, 128).T[:127]
    return mx_ref.matmul(mx_ref.quantize(e.reshape(128, 512).astype(BF)), (c.reshape(128, 8), np.full((16, 2), 127, np.uint8))).T.reshape(-1).astype(np.float64)
CODE_VALUE, SCALE_VALUE = values_of_codes(), 2.0 ** (np.arange(256) - 127.0)
def decode(q):
    return (CODE_VALUE[q[0]].reshape(16, 8, -1, 4) * SCALE_VALUE[q[1]][:, None, :, None] + 0.0).reshape(128, -1).astype(np.float32)
def f(rng, *shape):
    return mx_ref.flush((rng.standard_normal(shape, dtype=np.float32) * np.exp2(rng.integers(-2, 3, shape[:-1] + (1,)))).astype(BF))
def wide(rng, *shape, cols=0):
    v = rng.standard_normal(shape, dtype=np.float32) * np.exp2(rng.integers(-12, 13, shape)).astype(np.float32)
    if cols: v *= np.repeat(np.exp2(rng.integers(-cols, cols + 1, shape[:-2] + (1, shape[-1] // 4))) * (rng.random(shape[:-2] + (1, shape[-1] // 4)) > 0.0625), 4, axis=-1).astype(np.float32)
    return mx_ref.flush(v.astype(BF))
C, HALF, FAR = 448, 224, (2, 1)
def mate(r, t):
    return r ^ FAR[t]
def swap(s, t):
    lo, hi = np.arange(HALF), np.arange(HALF, C)
    return [join(pick(s[r], lo), pick(s[mate(r, t)], hi)) for r in range(N)]
def contend(e, p):
    a, b = p[:, ::2], p[:, 1::2]
    w = np.take_along_axis(e, b, axis=1) > np.take_along_axis(e, a, axis=1)
    l = np.empty_like(p)
    l[:, ::2] = np.where(w, b, a)
    l[:, 1::2] = np.where(w, a, b)
    return l
def layer(w, q):
    return [mx_ref.matmul(pick(w, np.arange(128 * b, 128 * b + 128)), q) for b in range(4)]
def clean(v):
    v = v.astype(np.float32)
    v[np.abs(v) < np.float32(2.0 ** -16)] = 0
    return v.astype(BF)
def numbers_of(rng):
    return {"x": clean(f(rng, N, 128, 4 * C)), "u": np.array(f(rng, N, 128, 512)), "v": np.array(f(rng, N, 128, 512))}
def wirings(rng):
    return {k: np.stack([gtable(np.stack([rng.permutation(C) for g in range(8)])) for r in range(N)]) for k in ("p0", "p1")}
def layers(rng, w, z):
    wc, ws = packed(np.stack([w] * N), rng)
    zc, zs = packed(np.stack([z] * N), rng)
    return {"wc": wc, "ws": ws, "zc": zc, "zs": zs}
def still(rng, k=1.0):
    w = np.zeros((128, 4, 128, 4), np.float32)
    i = np.arange(128)
    for b in range(4): w[i, b, i, b] = 32
    w = w.reshape(128, 2048)
    return layers(rng, w.astype(BF), (w * np.float32(k)).astype(BF))
def signs(rng):
    return np.stack([rng.permutation(8) % 2 * 2.0 - 1.0 for r in range(N)])
def pairs(rng, o):
    w = []
    for g in range(8):
        k = o[g].reshape(HALF, 2)[rng.permutation(HALF)]
        w.append(np.where(rng.integers(0, 2, (HALF, 1)) == 1, k[:, ::-1], k).reshape(-1))
    return np.stack(w)
def setup_inputs(rng):
    return {**numbers_of(rng), **wirings(rng), **layers(rng, np.array(f(rng, 128, 2048)), np.array(f(rng, 128, 2048)))}
def setup_inputs_ties(rng):
    d = numbers_of(rng)
    e = int(rng.integers(N))
    x = d["x"].reshape(N, 8, 16, C, 4)
    a = x[0][:, :8, :3].copy()
    a[:, :, 2] = 0
    for r in range(N):
        k = np.zeros(C, int) if r in (e, mate(e, 0)) else rng.permutation(C) % 3
        x[r][:, :8] = a[:, :, k]
    x[mate(e, 1)] = 0
    u = d["u"].reshape(N, 8, 16, 128, 4)
    for t in range(2): u[:, :, 8:, t::16] = 0
    w = np.array(f(rng, 128, 2048)).reshape(8, 16, 4, 8, 16, 4)
    w[:, 8:, :, :, :8] = 0
    return {"x": x.reshape(N, 128, 4 * C), "u": u.reshape(N, 128, 512), "v": d["v"], **wirings(rng), **layers(rng, w.reshape(128, 2048), np.array(f(rng, 128, 2048)))}
def setup_inputs_near(rng):
    d = numbers_of(rng)
    x = d["x"].astype(np.float32).reshape(N, 8, 16, C, 4)
    s = np.arange(C) // 2
    g = ((s[:, None] >> np.arange(8)) & 1) * np.exp2(np.arange(8) - 22.0)
    x[:, :, 0] = 0
    x[:, :, 0, :, 0] = 1
    x[:, :, 8] = g[:, :4]
    x[:, :, 9] = g[:, 4:]
    x[:, :, 10:] = rng.integers(4, 8, (N, 8, 6, C, 4)) * rng.choice([-1.0, 1.0], (N, 8, 6, C, 4)) * 2.0 ** -20
    one = int(rng.integers(8))
    x[:, one, 1:8] = 0
    x[:, one, 1, :, 0] = 1.75
    x[:, one, 2:4] = np.exp2(-np.arange(11.0, 19.0)).reshape(2, 1, 4)
    u = d["u"].reshape(N, 128, 128, 4)
    for t in range(2):
        u[:, :, t::16] = 0
        c = np.stack([np.exp2(-4.0 * rng.permutation(8)) for r in range(N)])
        k = (signs(rng) * c).astype(np.float32).astype(BF)
        c = c.astype(np.float32).astype(BF)
        for h in range(8):
            u[:, 16 * h, 16 * h + t, 0] = k[:, h]
            u[:, 16 * h + 8:16 * h + 10, 16 * h + t] = c[:, h][:, None, None]
    first = [pairs(rng, np.stack([np.roll(np.arange(C), -int(k)) for k in rng.permutation(8) % 2])) for r in range(N)]
    mixed = [s[contend(np.tile(s, (8, 1)), first[r])] + s for r in range(N)]
    second = []
    for r in range(N):
        k = np.concatenate([mixed[r][:, :HALF], mixed[mate(r, 1)][:, HALF:]], axis=1)
        second.append(pairs(rng, np.argsort(k, axis=1, kind="stable")))
    return {"x": x.reshape(N, 128, 4 * C).astype(BF), "u": u.reshape(N, 128, 512), "v": d["v"], "p0": np.stack([gtable(k) for k in first]), "p1": np.stack([gtable(k) for k in second]), **still(rng, 1.125)}
def setup_inputs_huge(rng):
    d = numbers_of(rng)
    x = 2.0 ** 30 * (0.6 + 0.4 * rng.random((N, 128, 4 * C)))
    u = d["u"].reshape(N, 128, 128, 4)
    for t in range(2):
        a = 2.0 ** 30 * (1 - 0.25 * rng.random((N, 128, 8, 4))) * signs(rng)[:, None, :, None]
        u[:, :, t::16] = a.astype(np.float32).astype(BF)
    return {"x": x.astype(np.float32).astype(BF), "u": u.reshape(N, 128, 512), "v": d["v"], **wirings(rng), **still(rng)}
def setup_inputs_spread(rng):
    d = setup_inputs(rng)
    d["x"] = clean(wide(rng, N, 128, 4 * C, cols=10))
    return d
def check_inputs(d):
    b = []
    for k in ("x", "u", "v"):
        a = np.abs(d[k].astype(np.float32))
        if not (np.isfinite(a).all() and ((a == 0) | (a >= 2.0 ** -30) & (a <= 2.0 ** 30)).all()): b.append("a value of " + k)
    for k in ("p0", "p1"):
        if any((np.sort(gentries(a), axis=1) != np.arange(C)).any() for a in d[k]): b.append("a group of " + k + " hasn't every number once")
    for k in ("wc", "zc"):
        if (d[k] != d[k][:1]).any(): b.append(k + " differs between ranks")
    for k in ("ws", "zs"):
        s = [mx_ref.live(p) for p in d[k]]
        if any((p != s[0]).any() for p in s): b.append(k + " differs between ranks")
    return b
def reference(x, u, v, p0, p1, wc, ws, zc, zs):
    w, z = pk(wc[0], ws[0]), pk(zc[0], zs[0])
    qu = [mx_ref.quantize(u[r]) for r in range(N)]
    now = [mx_ref.quantize(x[r]) for r in range(N)]
    kept = [[], []]
    for t in range(2):
        now = swap(now, t)
        for r in range(N):
            e = mx_ref.matmul(qu[r], now[r])[t::16] + np.float32(0.0)
            l = contend(e, gentries((p0, p1)[t][r]))
            kept[t].append(l)
            d = decode(now[r])
            p = ((gcols(d.astype(BF), l).astype(np.float32) + d) * np.float32(0.5)).astype(BF)
            now[r] = mx_ref.quantize(tile([np.maximum(a, np.float32(0.0)) * np.float32(0.03125) for a in layer(w, mx_ref.quantize(p))]))
    for t in (1, 0):
        for r in range(N):
            g = tile([a * np.float32(0.03125) for a in layer(z, now[r])])
            now[r] = mx_ref.quantize(gcols(g, np.argsort(kept[t][r], axis=1)))
        now = swap(now, t)
    y, ol = np.zeros((N, 128, C), np.float32), np.zeros((N, 8, 2 * C), np.float32)
    oc, osc = np.zeros((N, 128, 4 * C), np.uint8), np.zeros((N, 16, C), np.uint8)
    for r in range(N):
        y[r] = mx_ref.matmul(mx_ref.quantize(v[r]), now[r])
        ol[r] = np.concatenate([kept[0][r], kept[1][r]], axis=1)
        oc[r], osc[r] = emit(now[r])
    return {"y": y, "ol": ol, "oc": oc, "osc": osc}

@@ -1,0 +1,542 @@
+from concourse.mybir import dt, AluOpType, ActivationFunctionType
+
+C, H = 448, 224
+FAR = (2, 1)
+BIG = 16384.0
+LIFT = 16.0
+STEP = 0.03125
+F8, U8, BF, F32, I32, U16 = "float8_e4m3fn_x4", "uint8", "bfloat16", "float32", "int32", "uint16"
+
+SCRATCH = {}
+for _n, _w in (("xs", 4 * C), ("us", 512), ("vs", 512), ("em", 528), ("c16s", 16), ("c16", C), ("wb", C), ("sob", C),
+               ("dh0", 4 * C), ("dh1", 4 * C), ("pm0", 4 * C), ("pm1", 4 * C), ("hm0", 4 * C), ("hm1", 4 * C),
+               ("gm0", 4 * C), ("gm1", 4 * C), ("xm0", 4 * C), ("xm1", 4 * C), ("tmp0", 4 * H), ("tmp1", 4 * H),
+               ("dd0", 4 * H), ("dd1", 4 * H)):
+    SCRATCH[_n] = ("sbuf", [128, _w], BF)
+for _n, _w in (("iot", C), ("kk8", H), ("cf", 8), ("t1", 16), ("t2", 16), ("mk", 8), ("nmk", 8), ("cl", C), ("wsw", C + H),
+               ("prep0", C), ("prep1", C), ("soab", C), ("sol", C), ("soi", C), ("inv0", C), ("inv1", C),
+               ("dif0", 28), ("dif1", 28), ("pf0", 28), ("pf1", 28), ("basek", 28), ("t3", 28),
+               ("es0", C), ("es1", C), ("ga", H), ("lr", 2 * C), ("ys", C)):
+    SCRATCH[_n] = ("sbuf", [128, _w], F32)
+for _n, _w in (("ci", 8), ("uoi", 16), ("pt0", 28), ("pt1", 28), ("pp0", 28), ("pp1", 28), ("pin", 28), ("par", 28),
+               ("hlf", 28), ("base", 28), ("n1", 28), ("n2", 28), ("slot", 28)):
+    SCRATCH[_n] = ("sbuf", [128, _w], I32)
+for _n, _w in (("uo16", 16), ("i16", 28), ("p160", 28), ("p161", 28), ("ab0", 28), ("ab1", 28), ("l0", 28), ("l1", 28),
+               ("li0", 28), ("li1", 28), ("slot16", 28)):
+    SCRATCH[_n] = ("sbuf", [128, _w], U16)
+for _n, _w in (("e", 512), ("u", 128), ("ur", 256), ("v", 128), ("w", 512), ("z", 512), ("s0", C), ("s1", C), ("s3", C),
+               ("s4", C), ("o1", H), ("o2", H), ("o3", H), ("o4", H), ("p0", C), ("p1", C), ("h1", C)):
+    SCRATCH["q" + _n] = ("sbuf", [128, _w], F8)
+    SCRATCH["k" + _n] = ("sbuf", [128, _w], U8)
+for _b in range(8):
+    SCRATCH["ps%d" % _b] = ("psum", [128, 512], F32)
+
+POOL = ["a%d" % _i for _i in range(140)]
+SEMAPHORES = POOL + ["arr1", "arr2", "arr3", "arr4", "arr5", "snt1", "snt2", "snt3", "snt4"]
+
+
+def clash(a, b):
+    for na, ca in a:
+        for nb, cb in b:
+            if na == nb and not ca.isdisjoint(cb):
+                return True
+    return False
+
+
+def emit(ops, queues, T):
+    n = len(ops)
+    fixed = {}
+    known = {q: set() for q in queues}
+    at, waits = [], []
+    for i, o in enumerate(ops):
+        if o["fixed"]:
+            fixed.setdefault(o["fixed"], []).append(i)
+        if o["q"] is None:
+            at.append(set())
+            waits.append([])
+            continue
+        deps = set(o["after"])
+        for j in range(i):
+            p = ops[j]
+            if (clash(p["w"], o["r"] + o["w"] + o["x"]) or clash(p["r"] + p["x"], o["w"])
+                    or (p["q"] != o["q"] and clash(p["x"], o["x"]))):
+                deps.add(j)
+        kn = known[o["q"]]
+        need = [e for e in sorted(deps) if e not in kn and not any(e in at[d] for d in deps if d != e)]
+        mine = []
+        for e in need:
+            if e in kn:
+                continue
+            mine.append(e)
+            for m in (fixed[ops[e]["fixed"]] if ops[e]["fixed"] else [e]):
+                kn.add(m)
+                kn |= at[m]
+        at.append(set(kn))
+        waits.append(mine)
+    waiters = [[] for _ in range(n)]
+    for i in range(n):
+        for e in waits[i]:
+            waiters[e].append(i)
+    groups = {}
+    for e in range(n):
+        if waiters[e] and not ops[e]["fixed"]:
+            groups.setdefault((tuple(waiters[e]), ops[e]["inc"]), []).append(e)
+    used, sem_of = [], {}
+    for members in sorted(groups.values()):
+        inc = ops[members[0]]["inc"]
+        pick = None
+        for s in used:
+            if s["inc"] == inc and all(s["seen"] <= at[m] for m in members):
+                pick = s
+                break
+        if pick is None:
+            pick = {"name": POOL[len(used)], "inc": inc, "seen": set(), "count": 0}
+            used.append(pick)
+        pick["seen"].update(members)
+        pick["count"] += inc * len(members)
+        for m in members:
+            sem_of[m] = (pick["name"], pick["count"])
+    for name, members in fixed.items():
+        total = sum(ops[m]["inc"] for m in members)
+        for m in members:
+            sem_of[m] = (name, total)
+    for i, o in enumerate(ops):
+        if o["q"] is None:
+            continue
+        done = set()
+        for e in waits[i]:
+            if sem_of[e] not in done:
+                done.add(sem_of[e])
+                queues[o["q"]].wait_ge(T.sem[sem_of[e][0]], sem_of[e][1])
+        if o["fn"] is None:
+            continue
+        ins = o["fn"]()
+        if i in sem_of and not o["fixed"]:
+            ins.then_inc(T.sem[sem_of[i][0]], o["inc"])
+
+
+def rank_program(g, core, T, topo):
+    rank = T.rank_of(core)
+    if rank is None:
+        return
+    queues = {"V": g.vector, "S": g.scalar, "P": g.tensor, "G": g, "Y": g.sync}
+    ops = []
+    AF = ActivationFunctionType
+    OP = AluOpType
+
+    def view(name, lo=0, hi=None, step=1):
+        if hi is None:
+            hi = SCRATCH[name][1][1]
+        cols = {0} if name.startswith("ps") else set(range(lo, hi, step))
+        return {"ap": T[name][:, lo:hi:step] if step > 1 else T[name][:, lo:hi], "regs": [(name, cols)]}
+
+    def col(name, j):
+        return view(name, j, j + 1)
+
+    def by(win, off):
+        return {"ap": win["ap"].indirect(off["ap"]), "regs": win["regs"], "off": off["regs"]}
+
+    def add(q, fn, outs, ins, after=(), inc=1, fixed=None):
+        r, w, x = [], [], []
+        for v in outs:
+            w += v["regs"]
+            r += v.get("off", [])
+        for v in ins:
+            if isinstance(v, dict):
+                for reg in v["regs"]:
+                    (x if reg[0].startswith("ps") else r).append(reg)
+                r += v.get("off", [])
+        ops.append({"q": q, "fn": fn, "r": r, "w": w, "x": x, "after": list(after), "inc": inc, "fixed": fixed})
+        return len(ops) - 1
+
+    def val(s):
+        return s["ap"] if isinstance(s, dict) else s
+
+    def copy(out, in_):
+        return add("V", lambda: g.vector.tensor_copy(out["ap"], in_["ap"]), [out], [in_])
+
+    def ts(out, in0, s1, op0, s2=None, op1=None):
+        if op1 is None:
+            return add("V", lambda: g.vector.tensor_scalar(out["ap"], in0["ap"], val(s1), None, op0), [out], [in0, s1])
+        return add("V", lambda: g.vector.tensor_scalar(out["ap"], in0["ap"], val(s1), val(s2), op0, op1), [out], [in0, s1, s2])
+
+    def tt(out, in0, in1, op):
+        return add("V", lambda: g.vector.tensor_tensor(out["ap"], in0["ap"], in1["ap"], op), [out], [in0, in1])
+
+    def scan(out, d0, d1):
+        return add("V", lambda: g.vector.tensor_tensor_scan(out["ap"], d0["ap"], d1["ap"], 0.0, OP.mult, OP.add), [out], [d0, d1])
+
+    def act(out, in_, func, scale=None, bias=None):
+        kw = {}
+        if scale is not None:
+            kw["scale"] = val(scale)
+        if bias is not None:
+            kw["bias"] = val(bias)
+        return add("S", lambda: g.scalar.activation(out["ap"], in_["ap"], func, **kw), [out], [in_, scale, bias])
+
+    def quant(name, lo, n, tile):
+        q, k = view("q" + name, lo, lo + n), view("k" + name, lo, lo + n)
+        return add("V", lambda: g.vector.quantize_mx(q["ap"], k["ap"], tile["ap"]), [q, k], [tile])
+
+    def mm(bank, a, alo, b, blo, n=H):
+        o = view("ps%d" % bank, 0, n)
+        aq, ak = view("q" + a, alo, alo + 128), view("k" + a, alo, alo + 128)
+        bq, bk = view("q" + b, blo, blo + n), view("k" + b, blo, blo + n)
+        return add("P", lambda: g.tensor.matmul_mx(o["ap"], aq["ap"], ak["ap"], bq["ap"], bk["ap"], True, True), [o], [aq, ak, bq, bk])
+
+    def dma(q, out, in_, after=()):
+        outs = [out] if isinstance(out, dict) else []
+        return add(q, lambda: queues[q].dma_start(val(out), val(in_)), outs, [in_], after=after, inc=16)
+
+    def as_bytes(v):
+        return {"ap": v["ap"].bitcast(dt.uint8), "regs": v["regs"]}
+
+    def iota(out, pattern, base, mult, floats):
+        if floats:
+            return add("G", lambda: g.iota(out["ap"], pattern, base, mult, allow_small_or_imprecise_dtypes=True), [out], [])
+        return add("G", lambda: g.iota(out["ap"], pattern, base, mult), [out], [])
+
+    def send(k, t, land, apart=False):
+        d = FAR[t]
+        other = T.cores[rank + d if (rank // d) % 2 == 0 else rank - d]
+        rid, pid = topo.addr(other)[:2]
+        mask, count = topo.mask(core, other), len(topo.engines(core, other))
+        mine = []
+        for kind in ("q", "k"):
+            src, dst = view("%so%d" % (kind, k)), view(kind + land, H, C)
+            arr = "arr%d" % (k + 1 if apart and kind == "k" else k)
+            if kind == "q":
+                src, dst = as_bytes(src), as_bytes(dst)
+            mine.append(add("G", lambda s=src, o=dst, a=arr: g.remote_dma(o["ap"], s["ap"], T.sem[a], T.sem["snt%d" % k], pid, rid, mask),
+                            [], [src], inc=count, fixed="snt%d" % k))
+        if apart:
+            add(None, None, [view("q" + land, H, C)], [], inc=count, fixed="arr%d" % k)
+            add(None, None, [view("k" + land, H, C)], [], inc=count, fixed="arr%d" % (k + 1))
+        else:
+            add(None, None, [view("q" + land, H, C), view("k" + land, H, C)], [], inc=2 * count, fixed="arr%d" % k)
+        return mine
+
+    def psum(bank):
+        return view("ps%d" % bank, 0, H)
+
+    def plane(name, b, h=None):
+        if h is None:
+            return view(name, C * b, C * b + C)
+        return view(name, C * b + H * h, C * b + H * h + H)
+
+    def lane(name, b, h):
+        return view(name, 4 * H * h + b, 4 * H * h + 4 * H, 4)
+
+    def half(name, h):
+        return view(name, 4 * H * h, 4 * H * h + 4 * H)
+
+    def offs(name, h):
+        return view(name, 14 * h, 14 * h + 14)
+
+    def scaled(q, out, bank, relu):
+        if q == "S":
+            return act(out, psum(bank), AF.Relu if relu else AF.Copy, scale=STEP)
+        if relu:
+            return ts(out, psum(bank), 0.0, OP.max, STEP, OP.mult)
+        return ts(out, psum(bank), STEP, OP.mult)
+
+    def plain(q, out, in_):
+        return act(out, in_, AF.Copy) if q == "S" else copy(out, in_)
+
+    pcol, icol, i1col, selcol, invk, k0col, kcol = (col("cf", j) for j in (0, 2, 3, 4, 5, 6, 7))
+
+    def swapped(q, t, after=()):
+        for e in range(2):
+            dma(q, {"ap": T["pp%d" % t][e:128:2, :], "regs": [("pp%d" % t, {e})]}, T["p%d" % t][1 - e:128:2, :], after=after)
+
+    def steer(t):
+        for k in range(8):
+            act(view("cl", 2 * k + 1, C, 16), view("dif%d" % t), AF.Identity, scale=col("mk", k), bias=col("nmk", k))
+            act(view("wsw", 2 * k + 1, C, 16), view("pf%d" % t), AF.Identity, scale=col("mk", k))
+
+    def sides(t):
+        for e in range(2):
+            scan(view("soab", H * e, H * e + H), view("c16", 0, H), view("prep%d" % t, e, C, 2))
+        ts(view("ab%d" % t), view("soab", 15, C, 16), invk, OP.mult)
+
+    def products(t, h, state):
+        mm(4, "ur", 128 * t, state, H * h)
+        for b in range(4):
+            mm(b, "e", 128 * b, state, H * h)
+
+    def scores(q, t, h):
+        plain(q, view("es%d" % t, H * h, H * h + H), psum(4))
+
+    def halves(q, t, b, h):
+        plain(q, plane("dh%d" % t, b, h), psum(b))
+
+    def unpack(t, h, state, who):
+        products(t, h, state)
+        scores(who[0], t, h)
+        for b in range(4):
+            halves(who[1 + b], t, b, h)
+
+    part = {1: (6, 14), 0: (0, 6)}
+
+    def first(q, t, h):
+        a, b = part[h]
+        plain(q, view("ga", 16 * a, 16 * b), by(view("es%d" % t), view("ab%d" % t, a, b)))
+
+    def compare(t, h):
+        a, b = part[h]
+        tt(view("wsw", 32 * a, 32 * b, 2), by(view("es%d" % t), view("ab%d" % t, 14 + a, 14 + b)), view("ga", 16 * a, 16 * b), OP.is_gt)
+
+    def keep(h):
+        scan(view("sol", H * h, H * h + H), view("cl", H * h, H * h + H), view("wsw", H * h, H * h + H))
+
+    def listed(t, h):
+        ts(offs("l%d" % t, h), view("sol", H * h + 15, H * h + H, 16), 1.0 / LIFT, OP.mult)
+
+    def twin(q, t, b, h, at):
+        plain(q, view("dd%d" % t, H * at, H * at + H), psum(b) if q == "S" else plane("dh%d" % t, b, h))
+
+    def mix(t, b, h, at):
+        tt(lane("pm%d" % t, b, h), by(plane("dh%d" % t, b), offs("l%d" % t, h)), view("dd%d" % t, H * at, H * at + H), OP.add)
+
+    def fetch(t, b, h, at):
+        act(view("tmp%d" % t, H * at, H * at + H), by(plane("dh%d" % t, b), offs("l%d" % t, h)), AF.Copy)
+
+    def join(t, b, h, at):
+        tt(lane("pm%d" % t, b, h), view("tmp%d" % t, H * at, H * at + H), psum(b), OP.add)
+
+    def layer(a, state, h, bank):
+        for b in range(4):
+            mm(bank + b, a, 128 * b, state, H * h)
+
+    def undo(q, t, b, h):
+        plain(q, lane("xm%d" % t, b, h), by(plane("gm%d" % t, b), offs("li%d" % t, h)))
+
+    def setting(h):
+        act(view("wb", H * h, H * h + H), by(view("wsw"), offs("slot16", h)), AF.Copy)
+
+    def inverse(h, stage):
+        if stage == 0:
+            scan(view("sob", H * h, H * h + H), view("c16", 0, H), view("wb", H * h, H * h + H))
+        elif stage == 1:
+            tt(offs("t3", h), view("sob", H * h + 15, H * h + H, 16), offs("basek", h), OP.add)
+        else:
+            ts(offs("li1", h), offs("t3", h), invk, OP.mult)
+
+    def inverse0(h, stage):
+        if stage == 0:
+            scan(view("soi", H * h, H * h + H), view("c16", 0, H), view("inv0", H * h, H * h + H))
+        else:
+            ts(offs("li0", h), view("soi", H * h + 15, H * h + H, 16), invk, OP.mult)
+
+    dma("Y", view("xs", 4 * H, 4 * C), T.x[:, 4 * H:4 * C])
+    dma("Y", view("pt0"), T.p0[:, :])
+    dma("Y", view("pt1"), T.p1[:, :])
+    swapped("Y", 0)
+    dma("Y", view("us"), T.u[:, :])
+    dma("Y", view("xs", 0, 4 * H), T.x[:, 0:4 * H])
+    dma("Y", as_bytes(view("qw", 0, 256)), T.wc[:, 0:1024])
+    dma("Y", view("kw"), T.ws[:, :])
+
+    iota(view("ci", 0, 2), [[1, 2]], 0, 1, False)
+    iota(view("iot", 0, 128), [[1, 128]], 0, 0, True)
+    iota(view("uoi"), [[1, 2], [16, 8]], 0, 0, False)
+    iota(view("iot", 128, C), [[1, C - 128]], 128, 0, True)
+    iota(view("kk8"), [[0, 28], [1, 8]], 0, 0, True)
+    em = view("em")
+    add("V", lambda: g.vector.memset(em["ap"], 0.0), [em], [])
+    ts(view("ci", 2, 4), view("ci", 0, 2), 15, OP.bitwise_and)
+    ts(col("ci", 4), col("ci", 0), 15, OP.bitwise_and, 1, OP.logical_shift_right)
+    copy(view("cf", 0, 5), view("ci", 0, 5))
+    ts(view("t1"), view("iot", 0, 16), icol, OP.not_equal)
+    ts(view("t2"), view("iot", 0, 16), i1col, OP.is_equal, BIG - 1.0, OP.mult)
+    ts(view("i16"), view("iot", 0, 28), 0.0, OP.mult, icol, OP.add)
+    ts(view("em", 8, 520, 4), view("iot", 0, 128), pcol, OP.is_equal, 0.5, OP.mult)
+    tt(view("c16s"), view("t1"), view("t2"), OP.add)
+    act(view("c16"), by(view("c16s"), view("i16")), AF.Copy)
+    ts(view("mk"), view("iot", 0, 8), selcol, OP.is_equal, LIFT, OP.mult)
+    ts(view("nmk"), view("iot", 0, 8), selcol, OP.not_equal)
+    ts(invk, icol, 15.0, OP.is_equal, 1.0 / BIG, OP.max)
+    ts(k0col, icol, 15.0, OP.not_equal, BIG, OP.mult)
+    copy(view("uo16"), view("uoi"))
+    for b in range(4):
+        quant("e", 128 * b, 128, view("em", 8 - b, 520 - b))
+    ts(kcol, k0col, 1.0, OP.max)
+    ts(view("cl", 0, C, 2), view("kk8"), selcol, OP.not_equal)
+
+    quant("o1", 0, H, half("xs", 1))
+    sent1 = send(1, 0, "s0")
+    dma("Y", as_bytes(view("qw", 256, 512)), T.wc[:, 1024:2048], after=sent1)
+    swapped("Y", 1)
+    dma("Y", view("vs"), T.v[:, :])
+    copy(view("p160"), view("pt0"))
+    copy(view("p161"), view("pt1"))
+    act(view("prep0"), by(view("iot"), view("p160")), AF.Copy)
+    act(view("prep1"), by(view("iot"), view("p161")), AF.Copy)
+    tt(view("dif0"), view("pp0"), view("pt0"), OP.subtract)
+    copy(view("pf0"), view("pt0"))
+    copy(view("pf1"), view("pt1"))
+    quant("u", 0, 128, view("us"))
+    wq, wo, uo = view("qu"), view("qur"), view("uo16")
+    add("V", lambda: g.vector.tensor_copy(wo["ap"].bitcast(dt.uint32), wq["ap"].bitcast(dt.uint32).indirect(uo["ap"])), [wo], [wq, uo])
+    act(view("kur"), by(view("ku"), uo), AF.Copy)
+    steer(0)
+    sides(0)
+    quant("s0", 0, H, half("xs", 0))
+    unpack(0, 0, "s0", "SSSSS")
+    twin("S", 0, 0, 0, 2)
+    twin("S", 0, 1, 0, 3)
+    copy(by(view("inv1"), view("p161")), view("iot"))
+    scan(view("soi"), view("c16"), view("inv1"))
+    scan(view("soab", 0, H), view("c16", 0, H), view("prep1", 0, C, 2))
+    ts(view("pin"), view("soi", 15, C, 16), invk, OP.mult)
+    scan(view("soab", H, C), view("c16", 0, H), view("prep1", 1, C, 2))
+    ts(view("par"), view("pin"), 1, OP.bitwise_and)
+    ts(view("hlf"), view("pin"), 1, OP.logical_shift_right)
+    ts(view("ab1"), view("soab", 15, C, 16), invk, OP.mult)
+    tt(view("base"), view("pin"), view("par"), OP.subtract)
+    ts(view("n1"), view("hlf"), -1.0, OP.mult, float(C), OP.add)
+
+    products(0, 1, "s0")
+    scores("V", 0, 1)
+    for b in range(4):
+        halves("S", 0, b, 1)
+        if b < 2:
+            twin("S", 0, b, 1, b)
+    first("V", 0, 1)
+    compare(0, 1)
+    keep(1)
+    listed(0, 1)
+    fetch(0, 2, 1, 2)
+    fetch(0, 3, 1, 3)
+    mix(0, 0, 1, 0)
+    mix(0, 1, 1, 1)
+    join(0, 2, 1, 2)
+    join(0, 3, 1, 3)
+    first("S", 0, 0)
+    quant("p0", H, H, half("pm0", 1))
+    layer("w", "p0", 1, 4)
+    compare(0, 0)
+    for b in range(4):
+        scaled("SV"[b % 2], lane("hm0", b, 1), 4 + b, True)
+    quant("o2", 0, H, half("hm0", 1))
+    sent2 = send(2, 1, "s1")
+    dma("Y", as_bytes(view("qz")), T.zc[:, :], after=sent2)
+    dma("Y", view("kz"), T.zs[:, :])
+
+    for b in (2, 3):
+        mm(b, "e", 128 * b, "s0", 0)
+    keep(0)
+    tt(view("dif1"), view("pp1"), view("pt1"), OP.subtract)
+    listed(0, 0)
+    tt(view("n2"), view("n1"), view("par"), OP.mult)
+    fetch(0, 2, 0, 0)
+    fetch(0, 3, 0, 1)
+    steer(1)
+    mix(0, 0, 0, 2)
+    mix(0, 1, 0, 3)
+    join(0, 2, 0, 0)
+    join(0, 3, 0, 1)
+    tt(view("slot"), view("base"), view("n2"), OP.add)
+    quant("p0", 0, H, half("pm0", 0))
+    layer("w", "p0", 0, 4)
+    ts(view("basek"), view("base"), kcol, OP.mult)
+    copy(view("slot16"), view("slot"))
+    for b in range(4):
+        scaled("VS"[b % 2], lane("hm0", b, 0), 4 + b, True)
+    quant("s1", 0, H, half("hm0", 0))
+    unpack(1, 0, "s1", "VSVSV")
+    for b in range(4):
+        twin("SV"[b % 2], 1, b, 0, b)
+
+    products(1, 1, "s1")
+    scores("V", 1, 1)
+    halves("S", 1, 0, 1)
+    first("S", 1, 1)
+    halves("V", 1, 1, 1)
+    first("S", 1, 0)
+    compare(1, 1)
+    halves("S", 1, 2, 1)
+    compare(1, 0)
+    keep(1)
+    halves("S", 1, 3, 1)
+    keep(0)
+    listed(1, 1)
+    listed(1, 0)
+    for b in range(4):
+        fetch(1, b, 1, b)
+    act(view("wsw", C, C + H), view("wsw", 0, C, 2), AF.Identity, scale=-1.0, bias=1.0)
+    setting(1)
+    for b in range(4):
+        mix(1, b, 0, b)
+    quant("p1", 0, H, half("pm1", 0))
+    layer("w", "p1", 0, 4)
+    for b in range(4):
+        join(1, b, 1, b)
+    for b in range(4):
+        scaled("S", lane("hm1", b, 0), 4 + b, True)
+    quant("p1", H, H, half("pm1", 1))
+    layer("w", "p1", 1, 0)
+    inverse(1, 0)
+    quant("h1", 0, H, half("hm1", 0))
+    layer("z", "h1", 0, 4)
+    inverse(1, 1)
+    for b in range(4):
+        scaled("SV"[b % 2], lane("hm1", b, 1), b, True)
+    inverse(1, 2)
+    quant("h1", H, H, half("hm1", 1))
+    layer("z", "h1", 1, 0)
+    for b in range(4):
+        scaled("SSSV"[b], plane("gm1", b, 0), 4 + b, False)
+    for b in range(4):
+        scaled("SV"[b % 2], plane("gm1", b, 1), b, False)
+    for b in range(4):
+        undo("SV"[b % 2], 1, b, 1)
+    setting(0)
+    quant("o3", 0, H, half("xm1", 1))
+    sent3 = send(3, 1, "s3")
+
+    for stage in range(3):
+        inverse(0, stage)
+    for b in range(4):
+        undo("S", 1, b, 0)
+    copy(by(view("inv0"), view("l0")), view("iot"))
+    quant("s3", 0, H, half("xm1", 0))
+    layer("z", "s3", 0, 4)
+    inverse0(1, 0)
+    for b in range(3):
+        scaled("S", plane("gm0", b, 0), 4 + b, False)
+    inverse0(1, 1)
+    scaled("V", plane("gm0", 3, 0), 7, False)
+
+    layer("z", "s3", 1, 0)
+    for b in range(4):
+        scaled("SV"[b % 2], plane("gm0", b, 1), b, False)
+    for b in range(4):
+        undo("SV"[b % 2], 0, b, 1)
+    quant("o4", 0, H, half("xm0", 1))
+    sent4 = send(4, 0, "s4", apart=True)
+
+    act(view("lr", 0, C), by(view("iot"), view("l0")), AF.Copy)
+    inverse0(0, 0)
+    quant("v", 0, 128, view("vs"))
+    inverse0(0, 1)
+    for b in range(4):
+        undo("SV"[b % 2], 0, b, 0)
+    quant("s4", 0, H, half("xm0", 0))
+    mm(4, "v", 0, "s4", 0)
+    stores = [dma("Y", T.oc[:, 0:4 * H], as_bytes(view("qs4", 0, H)))]
+    act(view("lr", C, 2 * C), by(view("iot"), view("l1")), AF.Copy)
+    plain("V", view("ys", 0, H), psum(4))
+    stores.append(dma("Y", T.y[:, 0:H], view("ys", 0, H)))
+    stores.append(dma("Y", T.ol[:, :], {"ap": T.lr[0:128:16, :], "regs": view("lr")["regs"]}))
+
+    mm(5, "v", 0, "s4", H)
+    stores.append(dma("Y", T.oc[:, 4 * H:4 * C], as_bytes(view("qs4", H, C))))
+    for k in range(4):
+        rows = {"ap": T.ks4[32 * k:32 * k + 4, :], "regs": view("ks4")["regs"]}
+        stores.append(dma("YYSS"[k], T.osc[4 * k:4 * k + 4, :], rows))
+    plain("V", view("ys", H, C), psum(5))
+    stores.append(dma("S", T.y[:, H:C], view("ys", H, C)))
+    add("G", None, [], [], after=stores + sent1 + sent2 + sent3 + sent4)
+
+    emit(ops, queues, T)

@@ -13,15 +13,14 @@ for _n, _w in (("xs", 4 * C), ("us", 512), ("vs", 512), ("em", 528), ("c16s", 16
                ("gm0", 4 * C), ("gm1", 4 * C), ("xm0", 4 * C), ("xm1", 4 * C), ("tmp0", 4 * H), ("tmp1", 4 * H),
                ("dd0", 4 * H), ("dd1", 4 * H)):
     SCRATCH[_n] = ("sbuf", [128, _w], BF)
-for _n, _w in (("iot", C), ("kk8", H), ("cf", 8), ("t1", 16), ("t2", 16), ("mk", 8), ("nmk", 8), ("cl", C), ("wsw", C + H),
-               ("prep0", C), ("prep1", C), ("soab", C), ("sol", C), ("soi", C), ("inv0", C), ("inv1", C),
+for _n, _w in (("iot", C), ("kk8", H), ("cf", 8), ("t1", 16), ("t2", 16), ("mk", 8), ("nmk", 8), ("cl", C), ("wsw", C),
+               ("sol", C), ("soi", C), ("inv0", C), ("inv1", C),
                ("dif0", 28), ("dif1", 28), ("pf0", 28), ("pf1", 28), ("basek", 28), ("t3", 28),
-               ("es0", C), ("es1", C), ("ga", H), ("lr", 2 * C), ("ys", C)):
+               ("es0", C), ("es1", C), ("ga", C), ("lr", 2 * C), ("ys", C)):
     SCRATCH[_n] = ("sbuf", [128, _w], F32)
-for _n, _w in (("ci", 8), ("uoi", 16), ("pt0", 28), ("pt1", 28), ("pp0", 28), ("pp1", 28), ("pin", 28), ("par", 28),
-               ("hlf", 28), ("base", 28), ("n1", 28), ("n2", 28), ("slot", 28)):
+for _n, _w in (("ci", 8), ("uoi", 16), ("pt0", 28), ("pt1", 28), ("pp0", 28), ("pp1", 28), ("pin", 28), ("hlf", 28)):
     SCRATCH[_n] = ("sbuf", [128, _w], I32)
-for _n, _w in (("uo16", 16), ("i16", 28), ("p160", 28), ("p161", 28), ("ab0", 28), ("ab1", 28), ("l0", 28), ("l1", 28),
+for _n, _w in (("uo16", 16), ("i16", 28), ("p160", 28), ("p161", 28), ("l0", 28), ("l1", 28),
                ("li0", 28), ("li1", 28), ("slot16", 28)):
     SCRATCH[_n] = ("sbuf", [128, _w], U16)
 for _n, _w in (("e", 512), ("u", 128), ("ur", 256), ("v", 128), ("w", 512), ("z", 512), ("s0", C), ("s1", C), ("s3", C),
@@ -254,11 +253,6 @@ def rank_program(g, core, T, topo):
             act(view("cl", 2 * k + 1, C, 16), view("dif%d" % t), AF.Identity, scale=col("mk", k), bias=col("nmk", k))
             act(view("wsw", 2 * k + 1, C, 16), view("pf%d" % t), AF.Identity, scale=col("mk", k))
 
-    def sides(t):
-        for e in range(2):
-            scan(view("soab", H * e, H * e + H), view("c16", 0, H), view("prep%d" % t, e, C, 2))
-        ts(view("ab%d" % t), view("soab", 15, C, 16), invk, OP.mult)
-
     def products(t, h, state):
         mm(4, "ur", 128 * t, state, H * h)
         for b in range(4):
@@ -276,15 +270,11 @@ def rank_program(g, core, T, topo):
         for b in range(4):
             halves(who[1 + b], t, b, h)
 
-    part = {1: (6, 14), 0: (0, 6)}
-
     def first(q, t, h):
-        a, b = part[h]
-        plain(q, view("ga", 16 * a, 16 * b), by(view("es%d" % t), view("ab%d" % t, a, b)))
+        plain(q, view("ga", H * h, H * h + H), by(view("es%d" % t), offs("p16%d" % t, h)))
 
     def compare(t, h):
-        a, b = part[h]
-        tt(view("wsw", 32 * a, 32 * b, 2), by(view("es%d" % t), view("ab%d" % t, 14 + a, 14 + b)), view("ga", 16 * a, 16 * b), OP.is_gt)
+        tt(view("wsw", H * h, H * h + H, 2), view("ga", H * h + 1, H * h + H, 2), view("ga", H * h, H * h + H, 2), OP.is_gt)
 
     def keep(h):
         scan(view("sol", H * h, H * h + H), view("cl", H * h, H * h + H), view("wsw", H * h, H * h + H))
@@ -293,7 +283,11 @@ def rank_program(g, core, T, topo):
         ts(offs("l%d" % t, h), view("sol", H * h + 15, H * h + H, 16), 1.0 / LIFT, OP.mult)
 
     def twin(q, t, b, h, at):
-        plain(q, view("dd%d" % t, H * at, H * at + H), psum(b) if q == "S" else plane("dh%d" % t, b, h))
+        out, in_ = view("dd%d" % t, H * at, H * at + H), psum(b) if q == "S" else plane("dh%d" % t, b, h)
+        if q == "G":
+            add("G", lambda: g.affine_select(out["ap"], in_["ap"], [[0, H]], OP.is_ge, 0.0, 0, 0), [out], [in_])
+        else:
+            plain(q, out, in_)
 
     def mix(t, b, h, at):
         tt(lane("pm%d" % t, b, h), by(plane("dh%d" % t, b), offs("l%d" % t, h)), view("dd%d" % t, H * at, H * at + H), OP.add)
@@ -329,8 +323,8 @@ def rank_program(g, core, T, topo):
             ts(offs("li0", h), view("soi", H * h + 15, H * h + H, 16), invk, OP.mult)
 
     dma("Y", view("xs", 4 * H, 4 * C), T.x[:, 4 * H:4 * C])
-    dma("Y", view("pt0"), T.p0[:, :])
     dma("Y", view("pt1"), T.p1[:, :])
+    dma("Y", view("pt0"), T.p0[:, :])
     swapped("Y", 0)
     dma("Y", view("us"), T.u[:, :])
     dma("Y", view("xs", 0, 4 * H), T.x[:, 0:4 * H])
@@ -368,33 +362,25 @@ def rank_program(g, core, T, topo):
     dma("Y", as_bytes(view("qw", 256, 512)), T.wc[:, 1024:2048], after=sent1)
     swapped("Y", 1)
     dma("Y", view("vs"), T.v[:, :])
-    copy(view("p160"), view("pt0"))
     copy(view("p161"), view("pt1"))
-    act(view("prep0"), by(view("iot"), view("p160")), AF.Copy)
-    act(view("prep1"), by(view("iot"), view("p161")), AF.Copy)
     tt(view("dif0"), view("pp0"), view("pt0"), OP.subtract)
     copy(view("pf0"), view("pt0"))
-    copy(view("pf1"), view("pt1"))
+    copy(by(view("inv1"), offs("p161", 0)), view("iot", 0, H))
+    steer(0)
     quant("u", 0, 128, view("us"))
+    copy(view("p160"), view("pt0"))
     wq, wo, uo = view("qu"), view("qur"), view("uo16")
     add("V", lambda: g.vector.tensor_copy(wo["ap"].bitcast(dt.uint32), wq["ap"].bitcast(dt.uint32).indirect(uo["ap"])), [wo], [wq, uo])
     act(view("kur"), by(view("ku"), uo), AF.Copy)
-    steer(0)
-    sides(0)
     quant("s0", 0, H, half("xs", 0))
     unpack(0, 0, "s0", "SSSSS")
     twin("S", 0, 0, 0, 2)
     twin("S", 0, 1, 0, 3)
-    copy(by(view("inv1"), view("p161")), view("iot"))
+    copy(by(view("inv1"), offs("p161", 1)), view("iot", H, C))
+    copy(view("pf1"), view("pt1"))
     scan(view("soi"), view("c16"), view("inv1"))
-    scan(view("soab", 0, H), view("c16", 0, H), view("prep1", 0, C, 2))
     ts(view("pin"), view("soi", 15, C, 16), invk, OP.mult)
-    scan(view("soab", H, C), view("c16", 0, H), view("prep1", 1, C, 2))
-    ts(view("par"), view("pin"), 1, OP.bitwise_and)
-    ts(view("hlf"), view("pin"), 1, OP.logical_shift_right)
-    ts(view("ab1"), view("soab", 15, C, 16), invk, OP.mult)
-    tt(view("base"), view("pin"), view("par"), OP.subtract)
-    ts(view("n1"), view("hlf"), -1.0, OP.mult, float(C), OP.add)
+    ts(view("slot16"), view("soi", 15, C, 16), invk, OP.mult)
 
     products(0, 1, "s0")
     scores("V", 0, 1)
@@ -416,8 +402,10 @@ def rank_program(g, core, T, topo):
     quant("p0", H, H, half("pm0", 1))
     layer("w", "p0", 1, 4)
     compare(0, 0)
+    keep(0)
     for b in range(4):
         scaled("SV"[b % 2], lane("hm0", b, 1), 4 + b, True)
+    listed(0, 0)
     quant("o2", 0, H, half("hm0", 1))
     sent2 = send(2, 1, "s1")
     dma("Y", as_bytes(view("qz")), T.zc[:, :], after=sent2)
@@ -425,10 +413,7 @@ def rank_program(g, core, T, topo):
 
     for b in (2, 3):
         mm(b, "e", 128 * b, "s0", 0)
-    keep(0)
     tt(view("dif1"), view("pp1"), view("pt1"), OP.subtract)
-    listed(0, 0)
-    tt(view("n2"), view("n1"), view("par"), OP.mult)
     fetch(0, 2, 0, 0)
     fetch(0, 3, 0, 1)
     steer(1)
@@ -436,35 +421,32 @@ def rank_program(g, core, T, topo):
     mix(0, 1, 0, 3)
     join(0, 2, 0, 0)
     join(0, 3, 0, 1)
-    tt(view("slot"), view("base"), view("n2"), OP.add)
+    ts(view("hlf"), view("pin"), 1, OP.logical_shift_right)
     quant("p0", 0, H, half("pm0", 0))
     layer("w", "p0", 0, 4)
-    ts(view("basek"), view("base"), kcol, OP.mult)
-    copy(view("slot16"), view("slot"))
+    ts(view("basek"), view("hlf"), kcol, OP.mult, 2.0, OP.mult)
     for b in range(4):
         scaled("VS"[b % 2], lane("hm0", b, 0), 4 + b, True)
     quant("s1", 0, H, half("hm0", 0))
     unpack(1, 0, "s1", "VSVSV")
     for b in range(4):
-        twin("SV"[b % 2], 1, b, 0, b)
+        twin("G", 1, b, 0, b)
 
     products(1, 1, "s1")
     scores("V", 1, 1)
-    halves("S", 1, 0, 1)
     first("S", 1, 1)
-    halves("V", 1, 1, 1)
-    first("S", 1, 0)
-    compare(1, 1)
-    halves("S", 1, 2, 1)
+    first("V", 1, 0)
+    for b in range(4):
+        halves("S", 1, b, 1)
     compare(1, 0)
-    keep(1)
-    halves("S", 1, 3, 1)
+    compare(1, 1)
     keep(0)
-    listed(1, 1)
+    keep(1)
     listed(1, 0)
+    listed(1, 1)
     for b in range(4):
         fetch(1, b, 1, b)
-    act(view("wsw", C, C + H), view("wsw", 0, C, 2), AF.Identity, scale=-1.0, bias=1.0)
+    act(view("wsw", 1, C, 2), view("wsw", 0, C, 2), AF.Identity, scale=-1.0, bias=1.0)
     setting(1)
     for b in range(4):
         mix(1, b, 0, b)

@@ -2,26 +2,26 @@ from concourse.mybir import dt, AluOpType, ActivationFunctionType
 
 C, H = 448, 224
 FAR = (2, 1)
-BIG = 16384.0
-LIFT = 16.0
+BIG = 65536.0
 STEP = 0.03125
 F8, U8, BF, F32, I32, U16 = "float8_e4m3fn_x4", "uint8", "bfloat16", "float32", "int32", "uint16"
 
 SCRATCH = {}
-for _n, _w in (("xs", 4 * C), ("us", 512), ("vs", 512), ("em", 528), ("c16s", 16), ("c16", C), ("wb", C), ("sob", C),
+for _n, _w in (("xs", 4 * C), ("us", 512), ("vs", 512), ("em", 528), ("c16s", 16), ("c16", C), ("iot", C),
+               ("wb0", C), ("wb1", C), ("sob0", C), ("sob1", C), ("inv0", C), ("inv1", C), ("soi0", C), ("soi1", C),
                ("dh0", 4 * C), ("dh1", 4 * C), ("pm0", 4 * C), ("pm1", 4 * C), ("hm0", 4 * C), ("hm1", 4 * C),
-               ("gm0", 4 * C), ("gm1", 4 * C), ("xm0", 4 * C), ("xm1", 4 * C), ("tmp0", 4 * H), ("tmp1", 4 * H),
-               ("dd0", 4 * H), ("dd1", 4 * H)):
+               ("gm0", 4 * C), ("gm1", 4 * C), ("xm0", 4 * C), ("xm1", 4 * C), ("tmp0", 4 * C), ("tmp1", 4 * C),
+               ("dd0", 4 * C), ("dd1", 4 * C)):
     SCRATCH[_n] = ("sbuf", [128, _w], BF)
-for _n, _w in (("iot", C), ("kk8", H), ("cf", 8), ("t1", 16), ("t2", 16), ("mk", 8), ("nmk", 8), ("cl", C), ("wsw", C),
-               ("sol", C), ("soi", C), ("inv0", C), ("inv1", C),
-               ("dif0", 28), ("dif1", 28), ("pf0", 28), ("pf1", 28), ("basek", 28), ("t3", 28),
-               ("es0", C), ("es1", C), ("ga", C), ("lr", 2 * C), ("ys", C)):
+for _n, _w in (("cf", 12), ("t1", 32), ("t2", 32), ("cls", 16), ("cl0", C), ("cl1", C), ("wsw0", C), ("wsw1", C),
+               ("sol0", C), ("sol1", C), ("dif0", 28), ("dif1", 28), ("sgn0", 28), ("sgn1", 28), ("t30", 28), ("t31", 28),
+               ("t40", 28), ("t41", 28), ("es0", C), ("es1", C), ("ga0", C), ("ga1", C), ("lr", 2 * C), ("ys", C)):
     SCRATCH[_n] = ("sbuf", [128, _w], F32)
-for _n, _w in (("ci", 8), ("uoi", 16), ("pt0", 28), ("pt1", 28), ("pp0", 28), ("pp1", 28), ("pin", 28), ("hlf", 28)):
+for _n, _w in (("ci", 8), ("uoi", 16), ("pt0", 28), ("pt1", 28), ("pp0", 28), ("pp1", 28), ("pin0", 28), ("pin1", 28),
+               ("evn0", 28), ("evn1", 28), ("par0", 28), ("par1", 28)):
     SCRATCH[_n] = ("sbuf", [128, _w], I32)
 for _n, _w in (("uo16", 16), ("i16", 28), ("p160", 28), ("p161", 28), ("l0", 28), ("l1", 28),
-               ("li0", 28), ("li1", 28), ("slot16", 28)):
+               ("li0", 28), ("li1", 28), ("slot0", 28), ("slot1", 28)):
     SCRATCH[_n] = ("sbuf", [128, _w], U16)
 for _n, _w in (("e", 512), ("u", 128), ("ur", 256), ("v", 128), ("w", 512), ("z", 512), ("s0", C), ("s1", C), ("s3", C),
                ("s4", C), ("o1", H), ("o2", H), ("o3", H), ("o4", H), ("p0", C), ("p1", C), ("h1", C)):
@@ -30,8 +30,30 @@ for _n, _w in (("e", 512), ("u", 128), ("ur", 256), ("v", 128), ("w", 512), ("z"
 for _b in range(8):
     SCRATCH["ps%d" % _b] = ("psum", [128, 512], F32)
 
-POOL = ["a%d" % _i for _i in range(140)]
-SEMAPHORES = POOL + ["arr1", "arr2", "arr3", "arr4", "arr5", "snt1", "snt2", "snt3", "snt4"]
+POOL = ["a%d" % _i for _i in range(137)]
+SEMAPHORES = POOL + ["arr%d" % _i for _i in range(1, 6)] + ["snt%s%d" % (_k, _i) for _k in "qk" for _i in range(1, 5)]
+
+ORDER = """
+ici:G ci2:V lx1:Y iota:G iuo:G em0:V lu:Y lq0a:Y lp1:Y lq1a:Y ci3:V cf:V em1:V eq0:V lp0:Y lq0b:Y lq1b:Y invk:V i16:V
+ne0:V uo16:V ne1:V qe0:V qx1:V c16s:V qe3:V qu:V qe1:V eq1:V invk8:V p161:V qe2:V pq0:V pk0:S wz1:S pk1:S p160:V sca10:V
+cls:V c16:S lx0:Y sca11:V cl0:S dif0:V qx0:V md002:0 iotb:G sca12:V md003:1 md000:2 ms00:3 md001:4 wz0:S cl1:S pq1:V
+ed000:S cl150:V send1:G ms01:5 es00:S sca13:V ed003:V sci1:V es01:V tw003:V w150:V fst01:V md011:6 md010:7 md013:2
+md012:3 ed001:S lw0:Y lws:Y lz:Y lv:Y lzs:Y ed011:S tw011:V pin1:V ed010:S ed012:S fst00:S cmp01:V ed002:S evn1:V ed013:S
+tw001:V scn01:V cmp00:V tw010:G mr000:1 lst01:V mix011:V mix010:V fet012:S fet013:S joi012:V joi013:V scn00:V qp01:V
+lst00:V mix001:V mix003:V fet000:S fet002:S joj000:V joi002:V qp00:V lw1:Y mw003:5 re003:S dif1:V mw000:4 slot1:V re000:V
+cl151:V acol:V mw001:6 mw002:7 send2:G mw010:3 mw011:2 re001:S re011:S mw013:1 re013:S mw012:0 re002:V re010:V qh00:V
+re012:V qh01:V md100:5 md102:4 ms10:6 par1:V md101:2 ms11:1 md110:7 ed100:S ed102:S tw102:G md113:3 md112:0 es10:V
+md103:5 ed110:S mr112:4 w151:V es11:V ed101:V md111:6 fst10:V fst11:S sgn1:V tw100:V ed103:S mr110:7 ed112:S cmp10:V
+cmp11:V scn10:V ed111:S scn11:V ed113:S lst10:V tw101:V fet103:S lst11:V mix102:V mix100:V fet111:S mix101:V fet113:S
+joi103:V fet110:S joi111:V qp10:V fet112:S joi113:V joj110:V joj112:V set11:S mw100:1 qp11:V mw102:2 mw101:0 mw103:5
+re102:S re101:S re100:S scb11:V re103:V mw112:6 re112:V set10:S mw110:3 re110:S mw113:7 qh10:V mw111:4 re113:S mz100:2
+eg100:S re111:V scb10:V ia11:V mz103:0 qh11:V mz101:1 ia10:V ib11:V mz102:5 ib10:V mz110:6 mz113:3 mz111:7 mz112:2
+eg102:V ic11:V eg103:S eg101:S eg113:V ic10:V eg112:V eg110:S eg111:S un110:S un112:S un113:V un111:V qb11:V un102:S
+scl00:V un103:V scl01:V un101:S un100:S qb10:V send3:G mz001:4 mz002:5 mz000:0 eg002:S scl02:V mz003:1 eg003:S scl03:V
+eg001:V eg000:S scj01:V id01:V scj00:V mz010:3 eg010:S mz013:2 eg013:V mz011:6 id00:V mz012:7 eg011:S eg012:V un013:S
+un010:V un011:S un012:V qb01:V un003:S un001:S un000:S lr0:S send4:G un002:V lr1:V qb00:V oc0:Y ol:Y oc1:Y os0:Y qv:V
+my0:5 ey0:S os2:S os1:Y my2:1 os3:S oy0:Y my3:4 ey3:V ey2:S oy1:Y end:G
+"""
 
 
 def clash(a, b):
@@ -114,12 +136,10 @@ def emit(ops, queues, T):
             ins.then_inc(T.sem[sem_of[i][0]], o["inc"])
 
 
-def rank_program(g, core, T, topo):
+def plan(g, core, T, topo, order):
     rank = T.rank_of(core)
-    if rank is None:
-        return
     queues = {"V": g.vector, "S": g.scalar, "P": g.tensor, "G": g, "Y": g.sync}
-    ops = []
+    ops, step, bank, made, sent = [], {}, {}, {}, []
     AF = ActivationFunctionType
     OP = AluOpType
 
@@ -177,15 +197,16 @@ def rank_program(g, core, T, topo):
         q, k = view("q" + name, lo, lo + n), view("k" + name, lo, lo + n)
         return add("V", lambda: g.vector.quantize_mx(q["ap"], k["ap"], tile["ap"]), [q, k], [tile])
 
-    def mm(bank, a, alo, b, blo, n=H):
-        o = view("ps%d" % bank, 0, n)
+    def mm(at, a, alo, b, blo, n=H):
+        o = view("ps" + at, 0, n)
         aq, ak = view("q" + a, alo, alo + 128), view("k" + a, alo, alo + 128)
         bq, bk = view("q" + b, blo, blo + n), view("k" + b, blo, blo + n)
         return add("P", lambda: g.tensor.matmul_mx(o["ap"], aq["ap"], ak["ap"], bq["ap"], bk["ap"], True, True), [o], [aq, ak, bq, bk])
 
-    def dma(q, out, in_, after=()):
-        outs = [out] if isinstance(out, dict) else []
-        return add(q, lambda: queues[q].dma_start(val(out), val(in_)), outs, [in_], after=after, inc=16)
+    def dma(q, out, in_):
+        load = isinstance(out, dict)
+        return add(q, lambda: queues[q].dma_start(val(out), val(in_)), [out] if load else [], [in_],
+                   after=sent[-1] if sent and load else (), inc=16)
 
     def as_bytes(v):
         return {"ap": v["ap"].bitcast(dt.uint8), "regs": v["regs"]}
@@ -204,19 +225,24 @@ def rank_program(g, core, T, topo):
         for kind in ("q", "k"):
             src, dst = view("%so%d" % (kind, k)), view(kind + land, H, C)
             arr = "arr%d" % (k + 1 if apart and kind == "k" else k)
+            left = "snt%s%d" % (kind, k)
             if kind == "q":
                 src, dst = as_bytes(src), as_bytes(dst)
-            mine.append(add("G", lambda s=src, o=dst, a=arr: g.remote_dma(o["ap"], s["ap"], T.sem[a], T.sem["snt%d" % k], pid, rid, mask),
-                            [], [src], inc=count, fixed="snt%d" % k))
+            mine.append(add("G", lambda s=src, o=dst, a=arr, l=left: g.remote_dma(o["ap"], s["ap"], T.sem[a], T.sem[l], pid, rid, mask),
+                            [], [src], inc=count, fixed=left))
         if apart:
             add(None, None, [view("q" + land, H, C)], [], inc=count, fixed="arr%d" % k)
             add(None, None, [view("k" + land, H, C)], [], inc=count, fixed="arr%d" % (k + 1))
         else:
             add(None, None, [view("q" + land, H, C), view("k" + land, H, C)], [], inc=2 * count, fixed="arr%d" % k)
+        sent.append(mine)
         return mine
 
-    def psum(bank):
-        return view("ps%d" % bank, 0, H)
+    def psum(name, lo=0, hi=H):
+        return view("ps" + bank[name], lo, hi)
+
+    def part(name, h):
+        return view(name, H * h, H * h + H)
 
     def plane(name, b, h=None):
         if h is None:
@@ -232,293 +258,174 @@ def rank_program(g, core, T, topo):
     def offs(name, h):
         return view(name, 14 * h, 14 * h + 14)
 
-    def scaled(q, out, bank, relu):
+    def ends(name, h):
+        return view(name, H * h + 15, H * h + H, 16)
+
+    def scaled(q, out, in_, relu):
         if q == "S":
-            return act(out, psum(bank), AF.Relu if relu else AF.Copy, scale=STEP)
+            return act(out, in_, AF.Relu if relu else AF.Copy, scale=STEP)
         if relu:
-            return ts(out, psum(bank), 0.0, OP.max, STEP, OP.mult)
-        return ts(out, psum(bank), STEP, OP.mult)
+            return ts(out, in_, 0.0, OP.max, STEP, OP.mult)
+        return ts(out, in_, STEP, OP.mult)
 
     def plain(q, out, in_):
+        if q == "G":
+            return add("G", lambda: g.affine_select(out["ap"], in_["ap"], [[0, H]], OP.is_ge, 0.0, 0, 0), [out], [in_])
         return act(out, in_, AF.Copy) if q == "S" else copy(out, in_)
 
-    pcol, icol, i1col, selcol, invk, k0col, kcol = (col("cf", j) for j in (0, 2, 3, 4, 5, 6, 7))
+    def affine(q, out, in_, scale, bias=None):
+        if q == "S":
+            return act(out, in_, AF.Identity, scale=scale, bias=bias)
+        if bias is None:
+            return ts(out, in_, scale, OP.mult)
+        return ts(out, in_, scale, OP.mult, bias, OP.add)
 
-    def swapped(q, t, after=()):
-        for e in range(2):
-            dma(q, {"ap": T["pp%d" % t][e:128:2, :], "regs": [("pp%d" % t, {e})]}, T["p%d" % t][1 - e:128:2, :], after=after)
+    pcol, icol, i0col, invk, invk8, acol = (col("cf", j) for j in (0, 2, 3, 4, 5, 6))
+    run, before = view("iot", H, H + 16), view("iot", H - 1, H + 15)
 
-    def steer(t):
-        for k in range(8):
-            act(view("cl", 2 * k + 1, C, 16), view("dif%d" % t), AF.Identity, scale=col("mk", k), bias=col("nmk", k))
-            act(view("wsw", 2 * k + 1, C, 16), view("pf%d" % t), AF.Identity, scale=col("mk", k))
+    step["lx1"] = lambda q: dma(q, view("xs", 4 * H, 4 * C), T.x[:, 4 * H:4 * C])
+    step["lx0"] = lambda q: dma(q, view("xs", 0, 4 * H), T.x[:, 0:4 * H])
+    step["lu"] = lambda q: dma(q, view("us"), T.u[:, :])
+    step["lv"] = lambda q: dma(q, view("vs"), T.v[:, :])
+    step["lw0"] = lambda q: dma(q, as_bytes(view("qw", 0, 256)), T.wc[:, 0:1024])
+    step["lw1"] = lambda q: dma(q, as_bytes(view("qw", 256, 512)), T.wc[:, 1024:2048])
+    step["lws"] = lambda q: dma(q, view("kw"), T.ws[:, :])
+    step["lz"] = lambda q: dma(q, as_bytes(view("qz")), T.zc[:, :])
+    step["lzs"] = lambda q: dma(q, view("kz"), T.zs[:, :])
 
-    def products(t, h, state):
-        mm(4, "ur", 128 * t, state, H * h)
-        for b in range(4):
-            mm(b, "e", 128 * b, state, H * h)
-
-    def scores(q, t, h):
-        plain(q, view("es%d" % t, H * h, H * h + H), psum(4))
-
-    def halves(q, t, b, h):
-        plain(q, plane("dh%d" % t, b, h), psum(b))
-
-    def unpack(t, h, state, who):
-        products(t, h, state)
-        scores(who[0], t, h)
-        for b in range(4):
-            halves(who[1 + b], t, b, h)
-
-    def first(q, t, h):
-        plain(q, view("ga", H * h, H * h + H), by(view("es%d" % t), offs("p16%d" % t, h)))
-
-    def compare(t, h):
-        tt(view("wsw", H * h, H * h + H, 2), view("ga", H * h + 1, H * h + H, 2), view("ga", H * h, H * h + H, 2), OP.is_gt)
-
-    def keep(h):
-        scan(view("sol", H * h, H * h + H), view("cl", H * h, H * h + H), view("wsw", H * h, H * h + H))
-
-    def listed(t, h):
-        ts(offs("l%d" % t, h), view("sol", H * h + 15, H * h + H, 16), 1.0 / LIFT, OP.mult)
-
-    def twin(q, t, b, h, at):
-        out, in_ = view("dd%d" % t, H * at, H * at + H), psum(b) if q == "S" else plane("dh%d" % t, b, h)
-        if q == "G":
-            add("G", lambda: g.affine_select(out["ap"], in_["ap"], [[0, H]], OP.is_ge, 0.0, 0, 0), [out], [in_])
-        else:
-            plain(q, out, in_)
-
-    def mix(t, b, h, at):
-        tt(lane("pm%d" % t, b, h), by(plane("dh%d" % t, b), offs("l%d" % t, h)), view("dd%d" % t, H * at, H * at + H), OP.add)
-
-    def fetch(t, b, h, at):
-        act(view("tmp%d" % t, H * at, H * at + H), by(plane("dh%d" % t, b), offs("l%d" % t, h)), AF.Copy)
-
-    def join(t, b, h, at):
-        tt(lane("pm%d" % t, b, h), view("tmp%d" % t, H * at, H * at + H), psum(b), OP.add)
-
-    def layer(a, state, h, bank):
-        for b in range(4):
-            mm(bank + b, a, 128 * b, state, H * h)
-
-    def undo(q, t, b, h):
-        plain(q, lane("xm%d" % t, b, h), by(plane("gm%d" % t, b), offs("li%d" % t, h)))
-
-    def setting(h):
-        act(view("wb", H * h, H * h + H), by(view("wsw"), offs("slot16", h)), AF.Copy)
-
-    def inverse(h, stage):
-        if stage == 0:
-            scan(view("sob", H * h, H * h + H), view("c16", 0, H), view("wb", H * h, H * h + H))
-        elif stage == 1:
-            tt(offs("t3", h), view("sob", H * h + 15, H * h + H, 16), offs("basek", h), OP.add)
-        else:
-            ts(offs("li1", h), offs("t3", h), invk, OP.mult)
-
-    def inverse0(h, stage):
-        if stage == 0:
-            scan(view("soi", H * h, H * h + H), view("c16", 0, H), view("inv0", H * h, H * h + H))
-        else:
-            ts(offs("li0", h), view("soi", H * h + 15, H * h + H, 16), invk, OP.mult)
-
-    dma("Y", view("xs", 4 * H, 4 * C), T.x[:, 4 * H:4 * C])
-    dma("Y", view("pt1"), T.p1[:, :])
-    dma("Y", view("pt0"), T.p0[:, :])
-    swapped("Y", 0)
-    dma("Y", view("us"), T.u[:, :])
-    dma("Y", view("xs", 0, 4 * H), T.x[:, 0:4 * H])
-    dma("Y", as_bytes(view("qw", 0, 256)), T.wc[:, 0:1024])
-    dma("Y", view("kw"), T.ws[:, :])
-
-    iota(view("ci", 0, 2), [[1, 2]], 0, 1, False)
-    iota(view("iot", 0, 128), [[1, 128]], 0, 0, True)
-    iota(view("uoi"), [[1, 2], [16, 8]], 0, 0, False)
-    iota(view("iot", 128, C), [[1, C - 128]], 128, 0, True)
-    iota(view("kk8"), [[0, 28], [1, 8]], 0, 0, True)
     em = view("em")
-    add("V", lambda: g.vector.memset(em["ap"], 0.0), [em], [])
-    ts(view("ci", 2, 4), view("ci", 0, 2), 15, OP.bitwise_and)
-    ts(col("ci", 4), col("ci", 0), 15, OP.bitwise_and, 1, OP.logical_shift_right)
-    copy(view("cf", 0, 5), view("ci", 0, 5))
-    ts(view("t1"), view("iot", 0, 16), icol, OP.not_equal)
-    ts(view("t2"), view("iot", 0, 16), i1col, OP.is_equal, BIG - 1.0, OP.mult)
-    ts(view("i16"), view("iot", 0, 28), 0.0, OP.mult, icol, OP.add)
-    ts(view("em", 8, 520, 4), view("iot", 0, 128), pcol, OP.is_equal, 0.5, OP.mult)
-    tt(view("c16s"), view("t1"), view("t2"), OP.add)
-    act(view("c16"), by(view("c16s"), view("i16")), AF.Copy)
-    ts(view("mk"), view("iot", 0, 8), selcol, OP.is_equal, LIFT, OP.mult)
-    ts(view("nmk"), view("iot", 0, 8), selcol, OP.not_equal)
-    ts(invk, icol, 15.0, OP.is_equal, 1.0 / BIG, OP.max)
-    ts(k0col, icol, 15.0, OP.not_equal, BIG, OP.mult)
-    copy(view("uo16"), view("uoi"))
+    step["ici"] = lambda q: iota(view("ci", 0, 2), [[H, 2]], -H, 1, False)
+    step["iota"] = lambda q: iota(view("iot", 0, H + 16), [[1, H + 16]], -H, 0, True)
+    step["iotb"] = lambda q: iota(view("iot", H + 16, C), [[1, H - 16]], 16, 0, True)
+    step["iuo"] = lambda q: iota(view("uoi"), [[1, 2], [16, 8]], 0, 0, False)
+    step["em0"] = lambda q: add("V", lambda: g.vector.memset(em["ap"], 0.0), [em], [])
+    step["ci2"] = lambda q: ts(col("ci", 2), col("ci", 1), 15, OP.bitwise_and)
+    step["ci3"] = lambda q: ts(col("ci", 3), col("ci", 1), 14, OP.bitwise_and)
+    step["cf"] = lambda q: copy(view("cf", 0, 4), view("ci", 0, 4))
+    step["i16"] = lambda q: ts(view("i16"), view("iot", 0, 28), 0.0, OP.mult, icol, OP.add)
+    step["em1"] = lambda q: ts(view("em", 8, 520, 4), view("iot", 0, 128), pcol, OP.is_equal, 0.5, OP.mult)
+    for k, (at, name) in enumerate(((icol, "c16s"), (i0col, "cls"))):
+        a, b = view("t1", 16 * k, 16 * k + 16), view("t2", 16 * k, 16 * k + 16)
+        step["ne%d" % k] = lambda q, a=a, at=at: ts(a, run, at, OP.not_equal)
+        step["eq%d" % k] = lambda q, b=b, at=at: ts(b, before, at, OP.is_equal, BIG - 1.0, OP.mult)
+        step[name] = lambda q, a=a, b=b, name=name: tt(view(name), a, b, OP.add)
+    step["c16"] = lambda q: plain(q, view("c16"), by(view("c16s"), view("i16")))
+    step["invk"] = lambda q: ts(invk, icol, 15.0, OP.is_equal, 1.0 / BIG, OP.max)
+    step["invk8"] = lambda q: ts(invk8, i0col, 14.0, OP.is_equal, 1.0 / BIG, OP.max)
+    step["acol"] = lambda q: affine(q, acol, invk, -2.0)
+    step["uo16"] = lambda q: copy(view("uo16"), view("uoi"))
+    step["qu"] = lambda q: quant("u", 0, 128, view("us"))
+    step["qv"] = lambda q: quant("v", 0, 128, view("vs"))
     for b in range(4):
-        quant("e", 128 * b, 128, view("em", 8 - b, 520 - b))
-    ts(kcol, k0col, 1.0, OP.max)
-    ts(view("cl", 0, C, 2), view("kk8"), selcol, OP.not_equal)
+        step["qe%d" % b] = lambda q, b=b: quant("e", 128 * b, 128, view("em", 8 - b, 520 - b))
 
-    quant("o1", 0, H, half("xs", 1))
-    sent1 = send(1, 0, "s0")
-    dma("Y", as_bytes(view("qw", 256, 512)), T.wc[:, 1024:2048], after=sent1)
-    swapped("Y", 1)
-    dma("Y", view("vs"), T.v[:, :])
-    copy(view("p161"), view("pt1"))
-    tt(view("dif0"), view("pp0"), view("pt0"), OP.subtract)
-    copy(view("pf0"), view("pt0"))
-    copy(by(view("inv1"), offs("p161", 0)), view("iot", 0, H))
-    steer(0)
-    quant("u", 0, 128, view("us"))
-    copy(view("p160"), view("pt0"))
-    wq, wo, uo = view("qu"), view("qur"), view("uo16")
-    add("V", lambda: g.vector.tensor_copy(wo["ap"].bitcast(dt.uint32), wq["ap"].bitcast(dt.uint32).indirect(uo["ap"])), [wo], [wq, uo])
-    act(view("kur"), by(view("ku"), uo), AF.Copy)
-    quant("s0", 0, H, half("xs", 0))
-    unpack(0, 0, "s0", "SSSSS")
-    twin("S", 0, 0, 0, 2)
-    twin("S", 0, 1, 0, 3)
-    copy(by(view("inv1"), offs("p161", 1)), view("iot", H, C))
-    copy(view("pf1"), view("pt1"))
-    scan(view("soi"), view("c16"), view("inv1"))
-    ts(view("pin"), view("soi", 15, C, 16), invk, OP.mult)
-    ts(view("slot16"), view("soi", 15, C, 16), invk, OP.mult)
+    def pick(t):
+        wq, wo, uo = view("qu"), view("qur", 128 * t, 128 * t + 128), view("uo16", 8 * t, 8 * t + 8)
+        return add("V", lambda: g.vector.tensor_copy(wo["ap"].bitcast(dt.uint32), wq["ap"].bitcast(dt.uint32).indirect(uo["ap"])), [wo], [wq, uo])
 
-    products(0, 1, "s0")
-    scores("V", 0, 1)
-    for b in range(4):
-        halves("S", 0, b, 1)
-        if b < 2:
-            twin("S", 0, b, 1, b)
-    first("V", 0, 1)
-    compare(0, 1)
-    keep(1)
-    listed(0, 1)
-    fetch(0, 2, 1, 2)
-    fetch(0, 3, 1, 3)
-    mix(0, 0, 1, 0)
-    mix(0, 1, 1, 1)
-    join(0, 2, 1, 2)
-    join(0, 3, 1, 3)
-    first("S", 0, 0)
-    quant("p0", H, H, half("pm0", 1))
-    layer("w", "p0", 1, 4)
-    compare(0, 0)
-    keep(0)
-    for b in range(4):
-        scaled("SV"[b % 2], lane("hm0", b, 1), 4 + b, True)
-    listed(0, 0)
-    quant("o2", 0, H, half("hm0", 1))
-    sent2 = send(2, 1, "s1")
-    dma("Y", as_bytes(view("qz")), T.zc[:, :], after=sent2)
-    dma("Y", view("kz"), T.zs[:, :])
+    def stage(t):
+        s = str(t)
+        pt, pp, p16, wsw, cl, dh = "pt" + s, "pp" + s, "p16" + s, "wsw" + s, "cl" + s, "dh" + s
+        step["lp" + s] = lambda q: dma(q, view(pt), T["p" + s][:, :])
+        for e in range(2):
+            step["lq" + s + "ab"[e]] = lambda q, e=e: dma(q, {"ap": T[pp][e:128:2, :], "regs": [(pp, {e})]}, T["p" + s][1 - e:128:2, :])
+        both = {"ap": T[pp][:, :], "regs": [(pp, {0, 1})]}
+        step["pq" + s] = lambda q: pick(t)
+        step["pk" + s] = lambda q: plain(q, view("kur", 128 * t, 128 * t + 128), by(view("ku"), view("uo16", 8 * t, 8 * t + 8)))
+        step["p16" + s] = lambda q: copy(view(p16), view(pt))
+        step["cl" + s] = lambda q: plain(q, view(cl), by(view("cls"), view("i16")))
+        step["wz" + s] = lambda q: affine(q, view(wsw, 1, C, 2), view("iot", 0, H), 0.0)
+        step["dif" + s] = lambda q: tt(view("dif" + s), both, view(pt), OP.subtract)
+        step["cl15" + s] = lambda q: affine(q, view(cl, 15, C, 16), view("dif" + s), invk8)
+        step["w15" + s] = lambda q: copy(view(wsw, 15, C, 16), view(pt))
+        step["sci" + s] = lambda q: scan(view("soi" + s), view("c16"), view("inv" + s))
+        step["pin" + s] = lambda q: ts(view("pin" + s), view("soi" + s, 15, C, 16), invk, OP.mult, float(H), OP.add)
+        step["evn" + s] = lambda q: ts(view("evn" + s), view("pin" + s), 510, OP.bitwise_and)
+        step["slot" + s] = lambda q: copy(view("slot" + s), view("evn" + s))
+        step["par" + s] = lambda q: ts(view("par" + s), view("pin" + s), 1, OP.bitwise_and)
+        step["sgn" + s] = lambda q: ts(view("sgn" + s), view("par" + s), acol, OP.mult, invk, OP.add)
+        step["scl" + s] = lambda q: copy(by(view("inv" + s), view("l" + s)), view("iot"))
+        step["lr" + s] = lambda q: affine(q, view("lr", C * t, C * t + C), by(view("iot"), view("l" + s)), 1.0, float(H))
+        for h in range(2):
+            side(t, h, s, s + str(h), p16, wsw, cl, dh)
 
-    for b in (2, 3):
-        mm(b, "e", 128 * b, "s0", 0)
-    tt(view("dif1"), view("pp1"), view("pt1"), OP.subtract)
-    fetch(0, 2, 0, 0)
-    fetch(0, 3, 0, 1)
-    steer(1)
-    mix(0, 0, 0, 2)
-    mix(0, 1, 0, 3)
-    join(0, 2, 0, 0)
-    join(0, 3, 0, 1)
-    ts(view("hlf"), view("pin"), 1, OP.logical_shift_right)
-    quant("p0", 0, H, half("pm0", 0))
-    layer("w", "p0", 0, 4)
-    ts(view("basek"), view("hlf"), kcol, OP.mult, 2.0, OP.mult)
-    for b in range(4):
-        scaled("VS"[b % 2], lane("hm0", b, 0), 4 + b, True)
-    quant("s1", 0, H, half("hm0", 0))
-    unpack(1, 0, "s1", "VSVSV")
-    for b in range(4):
-        twin("G", 1, b, 0, b)
+    def side(t, h, s, n, p16, wsw, cl, dh):
+        state, back = ("s0", "s1")[t], ("s3", "h1")[t]
+        step["sca" + n] = lambda q: copy(by(view("inv" + s), offs(p16, h)), part("iot", h))
+        step["ms" + n] = lambda at: mm(at, "ur", 128 * t, state, H * h)
+        step["es" + n] = lambda q: plain(q, part("es" + s, h), psum("ms" + n))
+        step["fst" + n] = lambda q: plain(q, part("ga" + s, h), by(view("es" + s), offs(p16, h)))
+        step["cmp" + n] = lambda q: tt(view(wsw, H * h, H * h + H, 2), view("ga" + s, H * h + 1, H * h + H, 2), view("ga" + s, H * h, H * h + H, 2), OP.is_gt)
+        step["scn" + n] = lambda q: scan(part("sol" + s, h), part(cl, h), part(wsw, h))
+        step["lst" + n] = lambda q: copy(offs("l" + s, h), ends("sol" + s, h))
+        step["qp" + n] = lambda q: quant("o2", 0, H, half("pm0", 1)) if n == "01" else quant("p" + s, H * h, H, half("pm" + s, h))
+        step["qh" + n] = lambda q: quant(("s1", "h1")[t], H * h, H, half("hm" + s, h))
+        step["qb" + n] = lambda q: quant((("s4", "o4"), ("s3", "o3"))[t][h], 0, H, half("xm" + s, h))
+        step["set" + n] = lambda q: plain(q, part("wb" + s, h), by(view(wsw), offs("slot" + s, h)))
+        step["scb" + n] = lambda q: scan(part("sob" + s, h), view("c16", 0, H), part("wb" + s, h))
+        step["ia" + n] = lambda q: tt(offs("t3" + s, h), ends("sob" + s, h), offs("sgn" + s, h), OP.mult)
+        step["ib" + n] = lambda q: tt(offs("t4" + s, h), offs("t3" + s, h), offs("pin" + s, h), OP.add)
+        step["ic" + n] = lambda q: copy(offs("li" + s, h), offs("t4" + s, h))
+        step["scj" + n] = lambda q: scan(part("soi" + s, h), view("c16", 0, H), part("inv" + s, h))
+        step["id" + n] = lambda q: ts(offs("li" + s, h), ends("soi" + s, h), invk, OP.mult, float(H), OP.add)
+        for b in range(4):
+            cell(t, h, b, s, n + str(b), dh, state, back)
 
-    products(1, 1, "s1")
-    scores("V", 1, 1)
-    first("S", 1, 1)
-    first("V", 1, 0)
-    for b in range(4):
-        halves("S", 1, b, 1)
-    compare(1, 0)
-    compare(1, 1)
-    keep(0)
-    keep(1)
-    listed(1, 0)
-    listed(1, 1)
-    for b in range(4):
-        fetch(1, b, 1, b)
-    act(view("wsw", 1, C, 2), view("wsw", 0, C, 2), AF.Identity, scale=-1.0, bias=1.0)
-    setting(1)
-    for b in range(4):
-        mix(1, b, 0, b)
-    quant("p1", 0, H, half("pm1", 0))
-    layer("w", "p1", 0, 4)
-    for b in range(4):
-        join(1, b, 1, b)
-    for b in range(4):
-        scaled("S", lane("hm1", b, 0), 4 + b, True)
-    quant("p1", H, H, half("pm1", 1))
-    layer("w", "p1", 1, 0)
-    inverse(1, 0)
-    quant("h1", 0, H, half("hm1", 0))
-    layer("z", "h1", 0, 4)
-    inverse(1, 1)
-    for b in range(4):
-        scaled("SV"[b % 2], lane("hm1", b, 1), b, True)
-    inverse(1, 2)
-    quant("h1", H, H, half("hm1", 1))
-    layer("z", "h1", 1, 0)
-    for b in range(4):
-        scaled("SSSV"[b], plane("gm1", b, 0), 4 + b, False)
-    for b in range(4):
-        scaled("SV"[b % 2], plane("gm1", b, 1), b, False)
-    for b in range(4):
-        undo("SV"[b % 2], 1, b, 1)
-    setting(0)
-    quant("o3", 0, H, half("xm1", 1))
-    sent3 = send(3, 1, "s3")
+    def cell(t, h, b, s, n, dh, state, back):
+        win, to, tmp = by(plane(dh, b), offs("l" + s, h)), lane("pm" + s, b, h), plane("tmp" + s, b, h)
+        step["md" + n] = lambda at: mm(at, "e", 128 * b, state, H * h)
+        step["mr" + n] = step["md" + n]
+        step["ed" + n] = lambda q: plain(q, plane(dh, b, h), psum("md" + n))
+        step["tw" + n] = lambda q: plain(q, plane("dd" + s, b, h), plane(dh, b, h))
+        step["mix" + n] = lambda q: tt(to, win, plane("dd" + s, b, h), OP.add)
+        step["fet" + n] = lambda q: plain(q, tmp, win)
+        step["joi" + n] = lambda q: tt(to, tmp, psum("md" + n), OP.add)
+        step["joj" + n] = lambda q: tt(to, tmp, psum("mr" + n), OP.add)
+        step["mw" + n] = lambda at: mm(at, "w", 128 * b, "p" + s, H * h)
+        step["re" + n] = lambda q: scaled(q, lane("hm" + s, b, h), psum("mw" + n), True)
+        step["mz" + n] = lambda at: mm(at, "z", 128 * b, back, H * h)
+        step["eg" + n] = lambda q: scaled(q, plane("gm" + s, b, h), psum("mz" + n), False)
+        step["un" + n] = lambda q: plain(q, lane("xm" + s, b, h), by(plane("gm" + s, b), offs("li" + s, h)))
 
-    for stage in range(3):
-        inverse(0, stage)
-    for b in range(4):
-        undo("S", 1, b, 0)
-    copy(by(view("inv0"), view("l0")), view("iot"))
-    quant("s3", 0, H, half("xm1", 0))
-    layer("z", "s3", 0, 4)
-    inverse0(1, 0)
-    for b in range(3):
-        scaled("S", plane("gm0", b, 0), 4 + b, False)
-    inverse0(1, 1)
-    scaled("V", plane("gm0", 3, 0), 7, False)
+    stage(0)
+    stage(1)
+    for k, (lo, hi) in enumerate(((0, 8), (8, 14), (14, 22), (22, 28))):
+        step["scl0%d" % k] = lambda q, lo=lo, hi=hi: copy(by(view("inv0"), view("l0", lo, hi)), view("iot", 16 * lo, 16 * hi))
+        step["sca1%d" % k] = lambda q, lo=lo, hi=hi: copy(by(view("inv1"), view("p161", lo, hi)), view("iot", 16 * lo, 16 * hi))
+    step["qx1"] = lambda q: quant("o1", 0, H, half("xs", 1))
+    step["qx0"] = lambda q: quant("s0", 0, H, half("xs", 0))
+    step["send1"] = lambda q: send(1, 0, "s0")
+    step["send2"] = lambda q: send(2, 1, "p0")
+    step["send3"] = lambda q: send(3, 1, "s3")
+    step["send4"] = lambda q: send(4, 0, "s4", apart=True)
 
-    layer("z", "s3", 1, 0)
-    for b in range(4):
-        scaled("SV"[b % 2], plane("gm0", b, 1), b, False)
-    for b in range(4):
-        undo("SV"[b % 2], 0, b, 1)
-    quant("o4", 0, H, half("xm0", 1))
-    sent4 = send(4, 0, "s4", apart=True)
-
-    act(view("lr", 0, C), by(view("iot"), view("l0")), AF.Copy)
-    inverse0(0, 0)
-    quant("v", 0, 128, view("vs"))
-    inverse0(0, 1)
-    for b in range(4):
-        undo("SV"[b % 2], 0, b, 0)
-    quant("s4", 0, H, half("xm0", 0))
-    mm(4, "v", 0, "s4", 0)
-    stores = [dma("Y", T.oc[:, 0:4 * H], as_bytes(view("qs4", 0, H)))]
-    act(view("lr", C, 2 * C), by(view("iot"), view("l1")), AF.Copy)
-    plain("V", view("ys", 0, H), psum(4))
-    stores.append(dma("Y", T.y[:, 0:H], view("ys", 0, H)))
-    stores.append(dma("Y", T.ol[:, :], {"ap": T.lr[0:128:16, :], "regs": view("lr")["regs"]}))
-
-    mm(5, "v", 0, "s4", H)
-    stores.append(dma("Y", T.oc[:, 4 * H:4 * C], as_bytes(view("qs4", H, C))))
+    step["my0"] = lambda at: mm(at, "v", 0, "s4", 0)
+    step["ey0"] = lambda q: plain(q, part("ys", 0), psum("my0"))
+    for h in range(2):
+        step["oy%d" % h] = lambda q, h=h: dma(q, T.y[:, H * h:H * h + H], part("ys", h))
+        step["oc%d" % h] = lambda q, h=h: dma(q, T.oc[:, 4 * H * h:4 * H * h + 4 * H], as_bytes(part("qs4", h)))
+    step["my2"] = lambda at: mm(at, "v", 0, "s4", H, 128)
+    step["my3"] = lambda at: mm(at, "v", 0, "s4", C - 128, 128)
+    step["ey2"] = lambda q: plain(q, view("ys", H, H + 128), psum("my2", 0, 128))
+    step["ey3"] = lambda q: plain(q, view("ys", H + 128, C), psum("my3", 32, 128))
+    step["ol"] = lambda q: dma(q, T.ol[:, :], {"ap": T.lr[0:128:16, :], "regs": view("lr")["regs"]})
     for k in range(4):
-        rows = {"ap": T.ks4[32 * k:32 * k + 4, :], "regs": view("ks4")["regs"]}
-        stores.append(dma("YYSS"[k], T.osc[4 * k:4 * k + 4, :], rows))
-    plain("V", view("ys", H, C), psum(5))
-    stores.append(dma("S", T.y[:, H:C], view("ys", H, C)))
-    add("G", None, [], [], after=stores + sent1 + sent2 + sent3 + sent4)
+        step["os%d" % k] = lambda q, k=k: dma(q, T.osc[4 * k:4 * k + 4, :], {"ap": T.ks4[32 * k:32 * k + 4, :], "regs": view("ks4")["regs"]})
+    stores = ["oy0", "oy1", "oc0", "oc1", "ol", "os0", "os1", "os2", "os3"]
+    step["end"] = lambda q: add("G", None, [], [], after=[made[k] for k in stores] + sum(sent, []))
 
+    for word in order:
+        name, where = word.split(":")
+        bank[name] = where
+        lo = len(ops)
+        made[name] = step[name](where)
+        for o in ops[lo:]:
+            o["name"] = name
+    return ops, queues
+
+
+def rank_program(g, core, T, topo):
+    if T.rank_of(core) is None:
+        return
+    ops, queues = plan(g, core, T, topo, ORDER.split())
     emit(ops, queues, T)

from concourse.mybir import dt, AluOpType, ActivationFunctionType

C, H = 448, 224
FAR = (2, 1)
BIG = 65536.0
STEP = 0.03125
F8, U8, BF, F32, I32, U16 = "float8_e4m3fn_x4", "uint8", "bfloat16", "float32", "int32", "uint16"

SCRATCH = {}
for _n, _w in (("xs", 4 * C), ("us", 512), ("vs", 512), ("em", 528), ("c16s", 16), ("c16", C), ("iot", C),
               ("wb0", C), ("wb1", C), ("sob0", C), ("sob1", C), ("inv0", C), ("inv1", C), ("soi0", C), ("soi1", C),
               ("dh0", 4 * C), ("dh1", 4 * C), ("pm0", 4 * C), ("pm1", 4 * C), ("hm0", 4 * C), ("hm1", 4 * C),
               ("gm0", 4 * C), ("gm1", 4 * C), ("xm0", 4 * C), ("xm1", 4 * C), ("tmp0", 4 * C), ("tmp1", 4 * C),
               ("dd0", 4 * C), ("dd1", 4 * C)):
    SCRATCH[_n] = ("sbuf", [128, _w], BF)
for _n, _w in (("cf", 12), ("t1", 32), ("t2", 32), ("cls", 16), ("cl0", C), ("cl1", C), ("wsw0", C), ("wsw1", C),
               ("sol0", C), ("sol1", C), ("dif0", 28), ("dif1", 28), ("sgn0", 28), ("sgn1", 28), ("t30", 28), ("t31", 28),
               ("t40", 28), ("t41", 28), ("es0", C), ("es1", C), ("ga0", C), ("ga1", C), ("lr", 2 * C), ("ys", C)):
    SCRATCH[_n] = ("sbuf", [128, _w], F32)
for _n, _w in (("ci", 8), ("uoi", 16), ("pt0", 28), ("pt1", 28), ("pp0", 28), ("pp1", 28), ("pin0", 28), ("pin1", 28),
               ("evn0", 28), ("evn1", 28), ("par0", 28), ("par1", 28)):
    SCRATCH[_n] = ("sbuf", [128, _w], I32)
for _n, _w in (("uo16", 16), ("i16", 28), ("p160", 28), ("p161", 28), ("l0", 28), ("l1", 28),
               ("li0", 28), ("li1", 28), ("slot0", 28), ("slot1", 28)):
    SCRATCH[_n] = ("sbuf", [128, _w], U16)
for _n, _w in (("e", 512), ("u", 128), ("ur", 256), ("v", 128), ("w", 512), ("z", 512), ("s0", C), ("s1", C), ("s3", C),
               ("s4", C), ("o1", H), ("o2", H), ("o3", H), ("o4", H), ("p0", C), ("p1", C), ("h1", C)):
    SCRATCH["q" + _n] = ("sbuf", [128, _w], F8)
    SCRATCH["k" + _n] = ("sbuf", [128, _w], U8)
for _b in range(8):
    SCRATCH["ps%d" % _b] = ("psum", [128, 512], F32)

POOL = ["a%d" % _i for _i in range(137)]
SEMAPHORES = POOL + ["arr%d" % _i for _i in range(1, 6)] + ["snt%s%d" % (_k, _i) for _k in "qk" for _i in range(1, 5)]

ORDER = """
ici:G ci2:V lx1:Y iota:G iuo:G em0:V lu:Y lq0a:Y lp1:Y lq1a:Y ci3:V cf:V em1:V eq0:V lp0:Y lq0b:Y lq1b:Y invk:V i16:V
ne0:V uo16:V ne1:V qe0:V qx1:V c16s:V qe3:V qu:V qe1:V eq1:V invk8:V p161:V qe2:V pq0:V pk0:S wz1:S pk1:S p160:V sca10:V
cls:V c16:S lx0:Y sca11:V cl0:S dif0:V qx0:V md002:0 iotb:G sca12:V md003:1 md000:2 ms00:3 md001:4 wz0:S cl1:S pq1:V
ed000:S cl150:V send1:G ms01:5 es00:S sca13:V ed003:V sci1:V es01:V tw003:V w150:V fst01:V md011:6 md010:7 md013:2
md012:3 ed001:S lw0:Y lws:Y lz:Y lv:Y lzs:Y ed011:S tw011:V pin1:V ed010:S ed012:S fst00:S cmp01:V ed002:S evn1:V ed013:S
tw001:V scn01:V cmp00:V tw010:G mr000:1 lst01:V mix011:V mix010:V fet012:S fet013:S joi012:V joi013:V scn00:V qp01:V
lst00:V mix001:V mix003:V fet000:S fet002:S joj000:V joi002:V qp00:V lw1:Y mw003:5 re003:S dif1:V mw000:4 slot1:V re000:V
cl151:V acol:V mw001:6 mw002:7 send2:G mw010:3 mw011:2 re001:S re011:S mw013:1 re013:S mw012:0 re002:V re010:V qh00:V
re012:V qh01:V md100:5 md102:4 ms10:6 par1:V md101:2 ms11:1 md110:7 ed100:S ed102:S tw102:G md113:3 md112:0 es10:V
md103:5 ed110:S mr112:4 w151:V es11:V ed101:V md111:6 fst10:V fst11:S sgn1:V tw100:V ed103:S mr110:7 ed112:S cmp10:V
cmp11:V scn10:V ed111:S scn11:V ed113:S lst10:V tw101:V fet103:S lst11:V mix102:V mix100:V fet111:S mix101:V fet113:S
joi103:V fet110:S joi111:V qp10:V fet112:S joi113:V joj110:V joj112:V set11:S mw100:1 qp11:V mw102:2 mw101:0 mw103:5
re102:S re101:S re100:S scb11:V re103:V mw112:6 re112:V set10:S mw110:3 re110:S mw113:7 qh10:V mw111:4 re113:S mz100:2
eg100:S re111:V scb10:V ia11:V mz103:0 qh11:V mz101:1 ia10:V ib11:V mz102:5 ib10:V mz110:6 mz113:3 mz111:7 mz112:2
eg102:V ic11:V eg103:S eg101:S eg113:V ic10:V eg112:V eg110:S eg111:S un110:S un112:S un113:V un111:V qb11:V un102:S
scl00:V un103:V scl01:V un101:S un100:S qb10:V send3:G mz001:4 mz002:5 mz000:0 eg002:S scl02:V mz003:1 eg003:S scl03:V
eg001:V eg000:S scj01:V id01:V scj00:V mz010:3 eg010:S mz013:2 eg013:V mz011:6 id00:V mz012:7 eg011:S eg012:V un013:S
un010:V un011:S un012:V qb01:V un003:S un001:S un000:S lr0:S send4:G un002:V lr1:V qb00:V oc0:Y ol:Y oc1:Y os0:Y qv:V
my0:5 ey0:S os2:S os1:Y my2:1 os3:S oy0:Y my3:4 ey3:V ey2:S oy1:Y end:G
"""


def clash(a, b):
    for na, ca in a:
        for nb, cb in b:
            if na == nb and not ca.isdisjoint(cb):
                return True
    return False


def emit(ops, queues, T):
    n = len(ops)
    fixed = {}
    known = {q: set() for q in queues}
    at, waits = [], []
    for i, o in enumerate(ops):
        if o["fixed"]:
            fixed.setdefault(o["fixed"], []).append(i)
        if o["q"] is None:
            at.append(set())
            waits.append([])
            continue
        deps = set(o["after"])
        for j in range(i):
            p = ops[j]
            if (clash(p["w"], o["r"] + o["w"] + o["x"]) or clash(p["r"] + p["x"], o["w"])
                    or (p["q"] != o["q"] and clash(p["x"], o["x"]))):
                deps.add(j)
        kn = known[o["q"]]
        need = [e for e in sorted(deps) if e not in kn and not any(e in at[d] for d in deps if d != e)]
        mine = []
        for e in need:
            if e in kn:
                continue
            mine.append(e)
            for m in (fixed[ops[e]["fixed"]] if ops[e]["fixed"] else [e]):
                kn.add(m)
                kn |= at[m]
        at.append(set(kn))
        waits.append(mine)
    waiters = [[] for _ in range(n)]
    for i in range(n):
        for e in waits[i]:
            waiters[e].append(i)
    groups = {}
    for e in range(n):
        if waiters[e] and not ops[e]["fixed"]:
            groups.setdefault((tuple(waiters[e]), ops[e]["inc"]), []).append(e)
    used, sem_of = [], {}
    for members in sorted(groups.values()):
        inc = ops[members[0]]["inc"]
        pick = None
        for s in used:
            if s["inc"] == inc and all(s["seen"] <= at[m] for m in members):
                pick = s
                break
        if pick is None:
            pick = {"name": POOL[len(used)], "inc": inc, "seen": set(), "count": 0}
            used.append(pick)
        pick["seen"].update(members)
        pick["count"] += inc * len(members)
        for m in members:
            sem_of[m] = (pick["name"], pick["count"])
    for name, members in fixed.items():
        total = sum(ops[m]["inc"] for m in members)
        for m in members:
            sem_of[m] = (name, total)
    for i, o in enumerate(ops):
        if o["q"] is None:
            continue
        done = set()
        for e in waits[i]:
            if sem_of[e] not in done:
                done.add(sem_of[e])
                queues[o["q"]].wait_ge(T.sem[sem_of[e][0]], sem_of[e][1])
        if o["fn"] is None:
            continue
        ins = o["fn"]()
        if i in sem_of and not o["fixed"]:
            ins.then_inc(T.sem[sem_of[i][0]], o["inc"])


def plan(g, core, T, topo, order):
    rank = T.rank_of(core)
    queues = {"V": g.vector, "S": g.scalar, "P": g.tensor, "G": g, "Y": g.sync}
    ops, step, bank, made, sent = [], {}, {}, {}, []
    AF = ActivationFunctionType
    OP = AluOpType

    def view(name, lo=0, hi=None, step=1):
        if hi is None:
            hi = SCRATCH[name][1][1]
        cols = {0} if name.startswith("ps") else set(range(lo, hi, step))
        return {"ap": T[name][:, lo:hi:step] if step > 1 else T[name][:, lo:hi], "regs": [(name, cols)]}

    def col(name, j):
        return view(name, j, j + 1)

    def by(win, off):
        return {"ap": win["ap"].indirect(off["ap"]), "regs": win["regs"], "off": off["regs"]}

    def add(q, fn, outs, ins, after=(), inc=1, fixed=None):
        r, w, x = [], [], []
        for v in outs:
            w += v["regs"]
            r += v.get("off", [])
        for v in ins:
            if isinstance(v, dict):
                for reg in v["regs"]:
                    (x if reg[0].startswith("ps") else r).append(reg)
                r += v.get("off", [])
        ops.append({"q": q, "fn": fn, "r": r, "w": w, "x": x, "after": list(after), "inc": inc, "fixed": fixed})
        return len(ops) - 1

    def val(s):
        return s["ap"] if isinstance(s, dict) else s

    def copy(out, in_):
        return add("V", lambda: g.vector.tensor_copy(out["ap"], in_["ap"]), [out], [in_])

    def ts(out, in0, s1, op0, s2=None, op1=None):
        if op1 is None:
            return add("V", lambda: g.vector.tensor_scalar(out["ap"], in0["ap"], val(s1), None, op0), [out], [in0, s1])
        return add("V", lambda: g.vector.tensor_scalar(out["ap"], in0["ap"], val(s1), val(s2), op0, op1), [out], [in0, s1, s2])

    def tt(out, in0, in1, op):
        return add("V", lambda: g.vector.tensor_tensor(out["ap"], in0["ap"], in1["ap"], op), [out], [in0, in1])

    def scan(out, d0, d1):
        return add("V", lambda: g.vector.tensor_tensor_scan(out["ap"], d0["ap"], d1["ap"], 0.0, OP.mult, OP.add), [out], [d0, d1])

    def act(out, in_, func, scale=None, bias=None):
        kw = {}
        if scale is not None:
            kw["scale"] = val(scale)
        if bias is not None:
            kw["bias"] = val(bias)
        return add("S", lambda: g.scalar.activation(out["ap"], in_["ap"], func, **kw), [out], [in_, scale, bias])

    def quant(name, lo, n, tile):
        q, k = view("q" + name, lo, lo + n), view("k" + name, lo, lo + n)
        return add("V", lambda: g.vector.quantize_mx(q["ap"], k["ap"], tile["ap"]), [q, k], [tile])

    def mm(at, a, alo, b, blo, n=H):
        o = view("ps" + at, 0, n)
        aq, ak = view("q" + a, alo, alo + 128), view("k" + a, alo, alo + 128)
        bq, bk = view("q" + b, blo, blo + n), view("k" + b, blo, blo + n)
        return add("P", lambda: g.tensor.matmul_mx(o["ap"], aq["ap"], ak["ap"], bq["ap"], bk["ap"], True, True), [o], [aq, ak, bq, bk])

    def dma(q, out, in_):
        load = isinstance(out, dict)
        return add(q, lambda: queues[q].dma_start(val(out), val(in_)), [out] if load else [], [in_],
                   after=sent[-1] if sent and load else (), inc=16)

    def as_bytes(v):
        return {"ap": v["ap"].bitcast(dt.uint8), "regs": v["regs"]}

    def iota(out, pattern, base, mult, floats):
        if floats:
            return add("G", lambda: g.iota(out["ap"], pattern, base, mult, allow_small_or_imprecise_dtypes=True), [out], [])
        return add("G", lambda: g.iota(out["ap"], pattern, base, mult), [out], [])

    def send(k, t, land, apart=False):
        d = FAR[t]
        other = T.cores[rank + d if (rank // d) % 2 == 0 else rank - d]
        rid, pid = topo.addr(other)[:2]
        mask, count = topo.mask(core, other), len(topo.engines(core, other))
        mine = []
        for kind in ("q", "k"):
            src, dst = view("%so%d" % (kind, k)), view(kind + land, H, C)
            arr = "arr%d" % (k + 1 if apart and kind == "k" else k)
            left = "snt%s%d" % (kind, k)
            if kind == "q":
                src, dst = as_bytes(src), as_bytes(dst)
            mine.append(add("G", lambda s=src, o=dst, a=arr, l=left: g.remote_dma(o["ap"], s["ap"], T.sem[a], T.sem[l], pid, rid, mask),
                            [], [src], inc=count, fixed=left))
        if apart:
            add(None, None, [view("q" + land, H, C)], [], inc=count, fixed="arr%d" % k)
            add(None, None, [view("k" + land, H, C)], [], inc=count, fixed="arr%d" % (k + 1))
        else:
            add(None, None, [view("q" + land, H, C), view("k" + land, H, C)], [], inc=2 * count, fixed="arr%d" % k)
        sent.append(mine)
        return mine

    def psum(name, lo=0, hi=H):
        return view("ps" + bank[name], lo, hi)

    def part(name, h):
        return view(name, H * h, H * h + H)

    def plane(name, b, h=None):
        if h is None:
            return view(name, C * b, C * b + C)
        return view(name, C * b + H * h, C * b + H * h + H)

    def lane(name, b, h):
        return view(name, 4 * H * h + b, 4 * H * h + 4 * H, 4)

    def half(name, h):
        return view(name, 4 * H * h, 4 * H * h + 4 * H)

    def offs(name, h):
        return view(name, 14 * h, 14 * h + 14)

    def ends(name, h):
        return view(name, H * h + 15, H * h + H, 16)

    def scaled(q, out, in_, relu):
        if q == "S":
            return act(out, in_, AF.Relu if relu else AF.Copy, scale=STEP)
        if relu:
            return ts(out, in_, 0.0, OP.max, STEP, OP.mult)
        return ts(out, in_, STEP, OP.mult)

    def plain(q, out, in_):
        if q == "G":
            return add("G", lambda: g.affine_select(out["ap"], in_["ap"], [[0, H]], OP.is_ge, 0.0, 0, 0), [out], [in_])
        return act(out, in_, AF.Copy) if q == "S" else copy(out, in_)

    def affine(q, out, in_, scale, bias=None):
        if q == "S":
            return act(out, in_, AF.Identity, scale=scale, bias=bias)
        if bias is None:
            return ts(out, in_, scale, OP.mult)
        return ts(out, in_, scale, OP.mult, bias, OP.add)

    pcol, icol, i0col, invk, invk8, acol = (col("cf", j) for j in (0, 2, 3, 4, 5, 6))
    run, before = view("iot", H, H + 16), view("iot", H - 1, H + 15)

    step["lx1"] = lambda q: dma(q, view("xs", 4 * H, 4 * C), T.x[:, 4 * H:4 * C])
    step["lx0"] = lambda q: dma(q, view("xs", 0, 4 * H), T.x[:, 0:4 * H])
    step["lu"] = lambda q: dma(q, view("us"), T.u[:, :])
    step["lv"] = lambda q: dma(q, view("vs"), T.v[:, :])
    step["lw0"] = lambda q: dma(q, as_bytes(view("qw", 0, 256)), T.wc[:, 0:1024])
    step["lw1"] = lambda q: dma(q, as_bytes(view("qw", 256, 512)), T.wc[:, 1024:2048])
    step["lws"] = lambda q: dma(q, view("kw"), T.ws[:, :])
    step["lz"] = lambda q: dma(q, as_bytes(view("qz")), T.zc[:, :])
    step["lzs"] = lambda q: dma(q, view("kz"), T.zs[:, :])

    em = view("em")
    step["ici"] = lambda q: iota(view("ci", 0, 2), [[H, 2]], -H, 1, False)
    step["iota"] = lambda q: iota(view("iot", 0, H + 16), [[1, H + 16]], -H, 0, True)
    step["iotb"] = lambda q: iota(view("iot", H + 16, C), [[1, H - 16]], 16, 0, True)
    step["iuo"] = lambda q: iota(view("uoi"), [[1, 2], [16, 8]], 0, 0, False)
    step["em0"] = lambda q: add("V", lambda: g.vector.memset(em["ap"], 0.0), [em], [])
    step["ci2"] = lambda q: ts(col("ci", 2), col("ci", 1), 15, OP.bitwise_and)
    step["ci3"] = lambda q: ts(col("ci", 3), col("ci", 1), 14, OP.bitwise_and)
    step["cf"] = lambda q: copy(view("cf", 0, 4), view("ci", 0, 4))
    step["i16"] = lambda q: ts(view("i16"), view("iot", 0, 28), 0.0, OP.mult, icol, OP.add)
    step["em1"] = lambda q: ts(view("em", 8, 520, 4), view("iot", 0, 128), pcol, OP.is_equal, 0.5, OP.mult)
    for k, (at, name) in enumerate(((icol, "c16s"), (i0col, "cls"))):
        a, b = view("t1", 16 * k, 16 * k + 16), view("t2", 16 * k, 16 * k + 16)
        step["ne%d" % k] = lambda q, a=a, at=at: ts(a, run, at, OP.not_equal)
        step["eq%d" % k] = lambda q, b=b, at=at: ts(b, before, at, OP.is_equal, BIG - 1.0, OP.mult)
        step[name] = lambda q, a=a, b=b, name=name: tt(view(name), a, b, OP.add)
    step["c16"] = lambda q: plain(q, view("c16"), by(view("c16s"), view("i16")))
    step["invk"] = lambda q: ts(invk, icol, 15.0, OP.is_equal, 1.0 / BIG, OP.max)
    step["invk8"] = lambda q: ts(invk8, i0col, 14.0, OP.is_equal, 1.0 / BIG, OP.max)
    step["acol"] = lambda q: affine(q, acol, invk, -2.0)
    step["uo16"] = lambda q: copy(view("uo16"), view("uoi"))
    step["qu"] = lambda q: quant("u", 0, 128, view("us"))
    step["qv"] = lambda q: quant("v", 0, 128, view("vs"))
    for b in range(4):
        step["qe%d" % b] = lambda q, b=b: quant("e", 128 * b, 128, view("em", 8 - b, 520 - b))

    def pick(t):
        wq, wo, uo = view("qu"), view("qur", 128 * t, 128 * t + 128), view("uo16", 8 * t, 8 * t + 8)
        return add("V", lambda: g.vector.tensor_copy(wo["ap"].bitcast(dt.uint32), wq["ap"].bitcast(dt.uint32).indirect(uo["ap"])), [wo], [wq, uo])

    def stage(t):
        s = str(t)
        pt, pp, p16, wsw, cl, dh = "pt" + s, "pp" + s, "p16" + s, "wsw" + s, "cl" + s, "dh" + s
        step["lp" + s] = lambda q: dma(q, view(pt), T["p" + s][:, :])
        for e in range(2):
            step["lq" + s + "ab"[e]] = lambda q, e=e: dma(q, {"ap": T[pp][e:128:2, :], "regs": [(pp, {e})]}, T["p" + s][1 - e:128:2, :])
        both = {"ap": T[pp][:, :], "regs": [(pp, {0, 1})]}
        step["pq" + s] = lambda q: pick(t)
        step["pk" + s] = lambda q: plain(q, view("kur", 128 * t, 128 * t + 128), by(view("ku"), view("uo16", 8 * t, 8 * t + 8)))
        step["p16" + s] = lambda q: copy(view(p16), view(pt))
        step["cl" + s] = lambda q: plain(q, view(cl), by(view("cls"), view("i16")))
        step["wz" + s] = lambda q: affine(q, view(wsw, 1, C, 2), view("iot", 0, H), 0.0)
        step["dif" + s] = lambda q: tt(view("dif" + s), both, view(pt), OP.subtract)
        step["cl15" + s] = lambda q: affine(q, view(cl, 15, C, 16), view("dif" + s), invk8)
        step["w15" + s] = lambda q: copy(view(wsw, 15, C, 16), view(pt))
        step["sci" + s] = lambda q: scan(view("soi" + s), view("c16"), view("inv" + s))
        step["pin" + s] = lambda q: ts(view("pin" + s), view("soi" + s, 15, C, 16), invk, OP.mult, float(H), OP.add)
        step["evn" + s] = lambda q: ts(view("evn" + s), view("pin" + s), 510, OP.bitwise_and)
        step["slot" + s] = lambda q: copy(view("slot" + s), view("evn" + s))
        step["par" + s] = lambda q: ts(view("par" + s), view("pin" + s), 1, OP.bitwise_and)
        step["sgn" + s] = lambda q: ts(view("sgn" + s), view("par" + s), acol, OP.mult, invk, OP.add)
        step["scl" + s] = lambda q: copy(by(view("inv" + s), view("l" + s)), view("iot"))
        step["lr" + s] = lambda q: affine(q, view("lr", C * t, C * t + C), by(view("iot"), view("l" + s)), 1.0, float(H))
        for h in range(2):
            side(t, h, s, s + str(h), p16, wsw, cl, dh)

    def side(t, h, s, n, p16, wsw, cl, dh):
        state, back = ("s0", "s1")[t], ("s3", "h1")[t]
        step["sca" + n] = lambda q: copy(by(view("inv" + s), offs(p16, h)), part("iot", h))
        step["ms" + n] = lambda at: mm(at, "ur", 128 * t, state, H * h)
        step["es" + n] = lambda q: plain(q, part("es" + s, h), psum("ms" + n))
        step["fst" + n] = lambda q: plain(q, part("ga" + s, h), by(view("es" + s), offs(p16, h)))
        step["cmp" + n] = lambda q: tt(view(wsw, H * h, H * h + H, 2), view("ga" + s, H * h + 1, H * h + H, 2), view("ga" + s, H * h, H * h + H, 2), OP.is_gt)
        step["scn" + n] = lambda q: scan(part("sol" + s, h), part(cl, h), part(wsw, h))
        step["lst" + n] = lambda q: copy(offs("l" + s, h), ends("sol" + s, h))
        step["qp" + n] = lambda q: quant("o2", 0, H, half("pm0", 1)) if n == "01" else quant("p" + s, H * h, H, half("pm" + s, h))
        step["qh" + n] = lambda q: quant(("s1", "h1")[t], H * h, H, half("hm" + s, h))
        step["qb" + n] = lambda q: quant((("s4", "o4"), ("s3", "o3"))[t][h], 0, H, half("xm" + s, h))
        step["set" + n] = lambda q: plain(q, part("wb" + s, h), by(view(wsw), offs("slot" + s, h)))
        step["scb" + n] = lambda q: scan(part("sob" + s, h), view("c16", 0, H), part("wb" + s, h))
        step["ia" + n] = lambda q: tt(offs("t3" + s, h), ends("sob" + s, h), offs("sgn" + s, h), OP.mult)
        step["ib" + n] = lambda q: tt(offs("t4" + s, h), offs("t3" + s, h), offs("pin" + s, h), OP.add)
        step["ic" + n] = lambda q: copy(offs("li" + s, h), offs("t4" + s, h))
        step["scj" + n] = lambda q: scan(part("soi" + s, h), view("c16", 0, H), part("inv" + s, h))
        step["id" + n] = lambda q: ts(offs("li" + s, h), ends("soi" + s, h), invk, OP.mult, float(H), OP.add)
        for b in range(4):
            cell(t, h, b, s, n + str(b), dh, state, back)

    def cell(t, h, b, s, n, dh, state, back):
        win, to, tmp = by(plane(dh, b), offs("l" + s, h)), lane("pm" + s, b, h), plane("tmp" + s, b, h)
        step["md" + n] = lambda at: mm(at, "e", 128 * b, state, H * h)
        step["mr" + n] = step["md" + n]
        step["ed" + n] = lambda q: plain(q, plane(dh, b, h), psum("md" + n))
        step["tw" + n] = lambda q: plain(q, plane("dd" + s, b, h), plane(dh, b, h))
        step["mix" + n] = lambda q: tt(to, win, plane("dd" + s, b, h), OP.add)
        step["fet" + n] = lambda q: plain(q, tmp, win)
        step["joi" + n] = lambda q: tt(to, tmp, psum("md" + n), OP.add)
        step["joj" + n] = lambda q: tt(to, tmp, psum("mr" + n), OP.add)
        step["mw" + n] = lambda at: mm(at, "w", 128 * b, "p" + s, H * h)
        step["re" + n] = lambda q: scaled(q, lane("hm" + s, b, h), psum("mw" + n), True)
        step["mz" + n] = lambda at: mm(at, "z", 128 * b, back, H * h)
        step["eg" + n] = lambda q: scaled(q, plane("gm" + s, b, h), psum("mz" + n), False)
        step["un" + n] = lambda q: plain(q, lane("xm" + s, b, h), by(plane("gm" + s, b), offs("li" + s, h)))

    stage(0)
    stage(1)
    for k, (lo, hi) in enumerate(((0, 8), (8, 14), (14, 22), (22, 28))):
        step["scl0%d" % k] = lambda q, lo=lo, hi=hi: copy(by(view("inv0"), view("l0", lo, hi)), view("iot", 16 * lo, 16 * hi))
        step["sca1%d" % k] = lambda q, lo=lo, hi=hi: copy(by(view("inv1"), view("p161", lo, hi)), view("iot", 16 * lo, 16 * hi))
    step["qx1"] = lambda q: quant("o1", 0, H, half("xs", 1))
    step["qx0"] = lambda q: quant("s0", 0, H, half("xs", 0))
    step["send1"] = lambda q: send(1, 0, "s0")
    step["send2"] = lambda q: send(2, 1, "p0")
    step["send3"] = lambda q: send(3, 1, "s3")
    step["send4"] = lambda q: send(4, 0, "s4", apart=True)

    step["my0"] = lambda at: mm(at, "v", 0, "s4", 0)
    step["ey0"] = lambda q: plain(q, part("ys", 0), psum("my0"))
    for h in range(2):
        step["oy%d" % h] = lambda q, h=h: dma(q, T.y[:, H * h:H * h + H], part("ys", h))
        step["oc%d" % h] = lambda q, h=h: dma(q, T.oc[:, 4 * H * h:4 * H * h + 4 * H], as_bytes(part("qs4", h)))
    step["my2"] = lambda at: mm(at, "v", 0, "s4", H, 128)
    step["my3"] = lambda at: mm(at, "v", 0, "s4", C - 128, 128)
    step["ey2"] = lambda q: plain(q, view("ys", H, H + 128), psum("my2", 0, 128))
    step["ey3"] = lambda q: plain(q, view("ys", H + 128, C), psum("my3", 32, 128))
    step["ol"] = lambda q: dma(q, T.ol[:, :], {"ap": T.lr[0:128:16, :], "regs": view("lr")["regs"]})
    for k in range(4):
        step["os%d" % k] = lambda q, k=k: dma(q, T.osc[4 * k:4 * k + 4, :], {"ap": T.ks4[32 * k:32 * k + 4, :], "regs": view("ks4")["regs"]})
    stores = ["oy0", "oy1", "oc0", "oc1", "ol", "os0", "os1", "os2", "os3"]
    step["end"] = lambda q: add("G", None, [], [], after=[made[k] for k in stores] + sum(sent, []))

    for word in order:
        name, where = word.split(":")
        bank[name] = where
        lo = len(ops)
        made[name] = step[name](where)
        for o in ops[lo:]:
            o["name"] = name
    return ops, queues


def rank_program(g, core, T, topo):
    if T.rank_of(core) is None:
        return
    ops, queues = plan(g, core, T, topo, ORDER.split())
    emit(ops, queues, T)
